import numpy as np
import ml_dtypes


def mxq(x, axis, fmt="e4m3"):
    dtype, down = {"e4m3": (ml_dtypes.float8_e4m3fn, 7), "e5m2": (ml_dtypes.float8_e5m2, 14)}[fmt]
    v = np.moveaxis(np.asarray(x, np.float32).astype(ml_dtypes.bfloat16).astype(np.float64), axis, -1)
    blocks = v.reshape(v.shape[:-1] + (-1, 32))
    amax = np.abs(blocks).max(-1, keepdims=True)
    byte = np.maximum(np.where(amax > 0, np.frexp(amax)[1] - 1 + 127, 0) - down, 1)
    scale = np.exp2(byte - 127.0)
    codes = (blocks / scale).astype(np.float32).astype(dtype).astype(np.float64)
    return np.moveaxis((codes * scale).reshape(v.shape), -1, axis)


WIDE = False


def mx_kscale(k):
    if not WIDE:
        return np.ones(k)
    levels = np.array([10, -10, 5, -5, 0])
    if k % 512:
        return np.exp2(np.random.permutation(np.resize(levels, k // 32))).repeat(32)
    a = np.empty((k // 512, 16))
    for p in range(k // 512):
        a[p, :8] = np.random.permutation(np.resize(levels, 8))
        for g in range(8):
            far = levels[np.abs(levels - a[p, g]) >= 10]
            a[p, g + 8] = far[np.random.randint(len(far))]
    return np.exp2(a.ravel()).repeat(32)


def f64(x):
    return np.asarray(x).astype(np.float64)


def striped(idx):
    return np.tile(idx.reshape(-1, 16).T, (8, 1)).astype(np.uint16)


def unstriped(offs):
    return offs[:16].T.reshape(-1).astype(np.int64)


def pack_weight(w):
    k, n = w.shape
    w = f64(np.asarray(w, np.float32).astype(ml_dtypes.bfloat16)).reshape(k // 32, 32, n)
    amax = np.abs(w).max(1)
    byte = np.clip(np.where(amax > 0, np.frexp(amax)[1] - 1 + 127 - 7, 1), 1, 254)
    scaled = (w * np.exp2(127.0 - byte)[:, None, :]).reshape(k, n).astype(np.float32)
    words = np.ascontiguousarray(scaled.reshape(k // 512, 128, 4, n).transpose(0, 1, 3, 2)).astype(ml_dtypes.float8_e4m3fn).view(np.uint8)
    return words, np.ascontiguousarray(byte.astype(np.uint8).reshape(k // 512, 16, n))


def unpack_weight(words, scales):
    g, p, n, _ = words.shape
    vals = np.ascontiguousarray(words).view(ml_dtypes.float8_e4m3fn).astype(np.float64) * np.repeat(np.exp2(scales.astype(np.float64) - 127.0), 8, axis=1)[..., None]
    return vals.transpose(0, 1, 3, 2).reshape(g * 512, n)

def planes(y):
    n, m = y.shape
    v = y.astype(np.float32).astype(ml_dtypes.bfloat16).astype(np.float64).reshape(n // 32, 32, m)
    top = np.abs(v).max(1)
    byte = np.clip(np.where(top > 0, np.frexp(top)[1] - 1 + 127 - 7, 1), 1, 254)
    codes = (v * np.exp2(127.0 - byte)[:, None, :]).reshape(n, m).astype(np.float32).astype(ml_dtypes.float8_e4m3fn).view(np.uint8)
    words = codes.reshape(n // 512, 128, 4, m).transpose(0, 1, 3, 2)
    return np.ascontiguousarray(words), np.ascontiguousarray(byte.astype(np.uint8).reshape(n // 512, 16, m))


K, T, S, N = 512, 1024, 512, 512
P = 2 ** 7


def setup_inputs():
    n = np.random.standard_normal
    s = mx_kscale(K)[:, None]
    packed_xT = pack_weight(n((K, T)) * s)
    return {
        "x_words": packed_xT[0],
        "x_scales": packed_xT[1],
        "mean": np.tile(0.3 * np.random.standard_normal(T), (P, 1)).astype(np.float32),
        "inv": np.tile(np.random.uniform(0.5, 2.0, T), (P, 1)).astype(np.float32),
        "gsum": n((N, 1)).astype(np.float32),
        "b": (0.3 * n((N, 1))).astype(np.float32),
        "w1": (n((K, N)) / np.sqrt(K) / s).astype(np.float32),
        "offs": striped(np.random.permutation(T)[:S]),
    }


def reference(x_words, x_scales, mean, inv, gsum, b, w1, offs):
    xq = unpack_weight(x_words, x_scales)[:, unstriped(offs)]
    y = mxq(f64(w1), 0, "e4m3").T @ xq
    mg = f64(mean)[:1][:, unstriped(offs)]
    ig = f64(inv)[:1][:, unstriped(offs)]
    out_0 = (y - (f64(gsum) * mg)) * ig + f64(b)
    return (out_0,) + planes(out_0)

@@ -1,0 +1,220 @@
+from contextlib import ExitStack
+
+import concourse.mybir as mybir
+from concourse.masks import make_identity
+
+F32 = mybir.dt.float32
+BF16 = mybir.dt.bfloat16
+I32 = mybir.dt.int32
+U32 = mybir.dt.uint32
+U16 = mybir.dt.uint16
+U8 = mybir.dt.uint8
+FP8X4 = mybir.dt.float8_e4m3fn_x4
+ALU = mybir.AluOpType
+ACT = mybir.ActivationFunctionType
+
+K, T, S, N = 512, 1024, 512, 512
+P = 128
+PACK = 4
+CHUNK = 128
+CHUNKS = S // CHUNK
+W_PARTS = ((0, 128), (128, 256), (256, 384), (384, 512))
+MEAN_ROW, INV_ROW = 96, 112
+FLOPS = 2 * K * S * N
+BYTES = 4 * P * T + 16 * T + 2 * 4 * T + 2 * 4 * N + 4 * K * N + 2 * S * 8 + 4 * N * S + N * S + 16 * S
+
+
+def tile_picked_lnfold_none_po_kernel(
+    tc, x_words, x_scales, mean, inv, gsum, b, w1, offs, out_0, out_1, out_2
+):
+    nc = tc.nc
+    with ExitStack() as ctx:
+        sb = ctx.enter_context(tc.tile_pool(name="sb", bufs=1))
+        ps = ctx.enter_context(tc.psum_pool(name="ps", bufs=1))
+
+        offsets = sb.tile([P, S // 16], U16, name="offsets")
+        nc.sync.dma_start(offsets[:], offs)
+
+        stats = sb.tile([P, T], F32, name="stats", align_bytes=64)
+        nc.sync.dma_start(out=stats[MEAN_ROW:INV_ROW, :], in_=mean[MEAN_ROW:INV_ROW, :])
+        nc.scalar.dma_start(out=stats[INV_ROW:P, :], in_=inv[INV_ROW:P, :])
+
+        xs_all = sb.tile([P, T], U8, name="xs_all", tag="scales_in", align_bytes=64)
+        nc.vector.memset(xs_all[:].bitcast(I32), 0)
+        nc.vector.memset(stats[0:MEAN_ROW, :], 0.0)
+
+        xw_all = sb.tile([P, T], U32, name="xw_all", align_bytes=64)
+        nc.sync.dma_start(
+            out=xw_all[:].bitcast(I32),
+            in_=x_words[0].rearrange("p c r -> p (c r)").bitcast(I32),
+        )
+        for q in range(4):
+            queue = nc.scalar if q < 2 else nc.gpsimd
+            queue.dma_start(
+                out=xs_all[32 * q : 32 * q + 4, :].bitcast(I32),
+                in_=x_scales[0][4 * q : 4 * q + 4, :].bitcast(I32),
+            )
+
+        w_rows = w1.rearrange("(p j) c -> p j c", j=PACK)
+        w_raw = []
+        for part, (lo, hi) in enumerate(W_PARTS):
+            raw = sb.tile([P, PACK, hi - lo], F32, name="w_raw%d" % part, align_bytes=64)
+            nc.sync.dma_start(out=raw[:], in_=w_rows[:, :, lo:hi])
+            w_raw.append(raw)
+
+        g_cols = sb.tile([P, PACK], F32, name="g_cols")
+        b_cols = sb.tile([P, PACK], F32, name="b_cols")
+        nc.sync.dma_start(out=g_cols[:], in_=gsum.rearrange("(p t) o -> p (t o)", t=PACK))
+        nc.sync.dma_start(out=b_cols[:], in_=b.rearrange("(p t) o -> p (t o)", t=PACK))
+
+        ident = sb.tile([P, P], F32, name="ident", align_bytes=64)
+        make_identity(nc, ident[:])
+        signs = sb.tile([P, 2, CHUNKS], F32, name="signs")
+        nc.gpsimd.memset(signs[:, 0, :], -1.0)
+        nc.gpsimd.memset(signs[:, 1, :], 1.0)
+
+        stats_g = sb.tile([P, S], F32, name="stats_g", tag="picked", align_bytes=64)
+        nc.vector.tensor_copy(stats_g[:], stats[:].indirect(offsets[:]))
+        xw = sb.tile([P, S], U32, name="xw", align_bytes=64)
+        nc.vector.tensor_copy(xw[:], xw_all[:].indirect(offsets[:]))
+
+        w_bf = sb.tile([P, PACK, P, PACK], BF16, name="w_bf", align_bytes=64)
+
+        def cast_w(part):
+            lo, hi = W_PARTS[part]
+            nc.scalar.activation(
+                out=w_bf[:, :, lo // PACK : hi // PACK, :].rearrange("p t m j -> p m j t"),
+                in_=w_raw[part][:].rearrange("p j (m t) -> p m j t", t=PACK),
+                func=ACT.Copy,
+            )
+
+        cast_w(0)
+
+        turned = ps.tile([P, CHUNKS, P], F32, name="turned")
+        for c in range(CHUNKS):
+            nc.tensor.transpose(turned[:, c, :], stats_g[:, c * CHUNK : (c + 1) * CHUNK], ident[:])
+        stat_cols = sb.tile([P, 2, CHUNKS], F32, name="stat_cols")
+        nc.vector.tensor_tensor(
+            out=stat_cols[:],
+            in0=turned[:, :, MEAN_ROW : P : INV_ROW - MEAN_ROW].rearrange("p c s -> p s c"),
+            in1=signs[:],
+            op=ALU.mult,
+        )
+        inv_col = stat_cols[:, 1, :]
+        shift_col = sb.tile([P, CHUNKS], F32, name="shift_col")
+        nc.gpsimd.tensor_tensor(out=shift_col[:], in0=stat_cols[:, 0, :], in1=inv_col, op=ALU.mult)
+
+        xs = sb.tile([P, S], U8, name="xs", tag="picked", align_bytes=64)
+        nc.vector.tensor_copy(xs[:], xs_all[:].indirect(offsets[:]))
+
+        inv_ps = ps.tile([P, S], F32, name="inv_ps")
+        shift_ps = ps.tile([P, S], F32, name="shift_ps")
+        for c in range(CHUNKS):
+            nc.tensor.transpose(
+                inv_ps[:, c * CHUNK : (c + 1) * CHUNK], inv_col[:, c : c + 1].to_broadcast([P, P]), ident[:]
+            )
+        for c in range(CHUNKS):
+            nc.tensor.transpose(
+                shift_ps[:, c * CHUNK : (c + 1) * CHUNK], shift_col[:, c : c + 1].to_broadcast([P, P]), ident[:]
+            )
+
+        for part in range(1, len(W_PARTS)):
+            cast_w(part)
+
+        w_codes = sb.tile([P, N], U32, name="w_codes", align_bytes=64)
+        w_scales = sb.tile([P, N], U8, name="w_scales", tag="scales_in", align_bytes=64)
+        for t in range(PACK):
+            nc.vector.quantize_mx(
+                out=w_codes[:, t * P : (t + 1) * P].bitcast(FP8X4),
+                scales=w_scales[:, t * P : (t + 1) * P],
+                in_=w_bf[:, t, :, :].rearrange("p m j -> p (m j)"),
+            )
+
+        inv_rows = sb.tile([P, S], F32, name="inv_rows", align_bytes=64)
+        nc.vector.tensor_copy(out=inv_rows[:], in_=inv_ps[:])
+
+        y_codes = sb.tile([P, S], U32, name="y_codes", align_bytes=64)
+        y_scales = sb.tile([P, S], U8, name="y_scales", align_bytes=64)
+        out_rows = out_0.rearrange("(p t) j -> p t j", t=PACK)
+        out_words = out_1[0].rearrange("p c r -> p (c r)").bitcast(I32)
+
+        results = []
+        addends = []
+        scaleds = []
+
+        def product(c):
+            cols = slice(c * CHUNK, (c + 1) * CHUNK)
+            acc = ps.tile([P, PACK, CHUNK], F32, name="acc%d" % c)
+            for t in range(PACK):
+                nc.tensor.matmul_mx(
+                    out=acc[:, t, :],
+                    lhsT=w_codes[:, t * P : (t + 1) * P].bitcast(FP8X4),
+                    lhsT_scale=w_scales[:, t * P : (t + 1) * P],
+                    rhs=xw[:, cols].bitcast(FP8X4),
+                    rhs_scale=xs[:, cols],
+                    start=True,
+                    stop=True,
+                )
+            addend = sb.tile([P, PACK, CHUNK], F32, name="addend%d" % c, align_bytes=64)
+            for t in range(PACK):
+                nc.scalar.activation(
+                    out=addend[:, t, :],
+                    in_=shift_ps[:, cols],
+                    func=ACT.Identity,
+                    scale=g_cols[:, t : t + 1],
+                    bias=b_cols[:, t : t + 1],
+                )
+            scaled = sb.tile([P, PACK, CHUNK], F32, name="scaled%d" % c, align_bytes=64)
+            nc.vector.tensor_tensor(
+                out=scaled[:],
+                in0=acc[:],
+                in1=inv_rows[:, cols].unsqueeze(1).to_broadcast([P, PACK, CHUNK]),
+                op=ALU.mult,
+            )
+            addends.append(addend)
+            scaleds.append(scaled)
+
+        def finish(c):
+            cols = slice(c * CHUNK, (c + 1) * CHUNK)
+            result = sb.tile([P, PACK, CHUNK], F32, name="result%d" % c, align_bytes=64)
+            nc.vector.tensor_tensor(out=result[:], in0=scaleds[c][:], in1=addends[c][:], op=ALU.add)
+            nc.sync.dma_start(out=out_rows[:, :, cols], in_=result[:])
+            results.append(result)
+
+        roundeds = []
+
+        def round_result(c):
+            rounded = sb.tile([P, CHUNK, PACK], BF16, name="rounded%d" % c, align_bytes=64)
+            dst = rounded[:].rearrange("p (c i) t -> p c t i", i=4)
+            src = results[c][:].rearrange("p t (c i) -> p c t i", i=4)
+            if c == CHUNKS - 1:
+                nc.vector.tensor_copy(out=dst, in_=src)
+            else:
+                nc.scalar.copy(out=dst, in_=src)
+            roundeds.append(rounded)
+
+        def planes(c):
+            cols = slice(c * CHUNK, (c + 1) * CHUNK)
+            rounded = roundeds[c]
+            nc.vector.quantize_mx(
+                out=y_codes[:, cols].bitcast(FP8X4),
+                scales=y_scales[:, cols],
+                in_=rounded[:].rearrange("p c t -> p (c t)"),
+            )
+            nc.sync.dma_start(out=out_words[:, cols], in_=y_codes[:, cols].bitcast(I32))
+
+        for step in range(CHUNKS + 2):
+            if step < CHUNKS:
+                product(step)
+            if 0 <= step - 1 < CHUNKS:
+                finish(step - 1)
+            if 0 <= step - 2 < CHUNKS:
+                planes(step - 2)
+            if 0 <= step - 1 < CHUNKS:
+                round_result(step - 1)
+        for q in range(4):
+            queue = nc.sync if q % 2 == 0 else nc.scalar
+            queue.dma_start(
+                out=out_2[0][4 * q : 4 * q + 4, :].bitcast(I32),
+                in_=y_scales[32 * q : 32 * q + 4, :].bitcast(I32),
+            )

@@ -18,7 +18,9 @@ P = 128
 PACK = 4
 CHUNK = 128
 CHUNKS = S // CHUNK
-W_PARTS = ((0, 128), (128, 256), (256, 384), (384, 512))
+HALF = S // 2
+DIRECT = CHUNKS // 2
+W_PARTS = ((0, 192), (192, 384), (384, 512))
 MEAN_ROW, INV_ROW = 96, 112
 FLOPS = 2 * K * S * N
 BYTES = 4 * P * T + 16 * T + 2 * 4 * T + 2 * 4 * N + 4 * K * N + 2 * S * 8 + 4 * N * S + N * S + 16 * S
@@ -30,16 +32,18 @@ def tile_picked_lnfold_none_po_kernel(
     nc = tc.nc
     with ExitStack() as ctx:
         sb = ctx.enter_context(tc.tile_pool(name="sb", bufs=1))
+        reuse = ctx.enter_context(tc.tile_pool(name="reuse", bufs=1))
         ps = ctx.enter_context(tc.psum_pool(name="ps", bufs=1))
 
         offsets = sb.tile([P, S // 16], U16, name="offsets")
         nc.sync.dma_start(offsets[:], offs)
+        half_offsets = [offsets[:, h * HALF // 16 : (h + 1) * HALF // 16] for h in range(2)]
 
         stats = sb.tile([P, T], F32, name="stats", align_bytes=64)
         nc.sync.dma_start(out=stats[MEAN_ROW:INV_ROW, :], in_=mean[MEAN_ROW:INV_ROW, :])
         nc.scalar.dma_start(out=stats[INV_ROW:P, :], in_=inv[INV_ROW:P, :])
 
-        xs_all = sb.tile([P, T], U8, name="xs_all", tag="scales_in", align_bytes=64)
+        xs_all = sb.tile([P, T], U8, name="xs_all", align_bytes=64)
         nc.vector.memset(xs_all[:].bitcast(I32), 0)
         nc.vector.memset(stats[0:MEAN_ROW, :], 0.0)
 
@@ -48,16 +52,16 @@ def tile_picked_lnfold_none_po_kernel(
             out=xw_all[:].bitcast(I32),
             in_=x_words[0].rearrange("p c r -> p (c r)").bitcast(I32),
         )
-        for q in range(4):
-            queue = nc.scalar if q < 2 else nc.gpsimd
-            queue.dma_start(
-                out=xs_all[32 * q : 32 * q + 4, :].bitcast(I32),
-                in_=x_scales[0][4 * q : 4 * q + 4, :].bitcast(I32),
-            )
 
         w_rows = w1.rearrange("(p j) c -> p j c", j=PACK)
         w_raw = []
         for part, (lo, hi) in enumerate(W_PARTS):
+            if part == len(W_PARTS) - 1:
+                for q in range(4):
+                    nc.sync.dma_start(
+                        out=xs_all[32 * q : 32 * q + 4, :].bitcast(I32),
+                        in_=x_scales[0][4 * q : 4 * q + 4, :].bitcast(I32),
+                    )
             raw = sb.tile([P, PACK, hi - lo], F32, name="w_raw%d" % part, align_bytes=64)
             nc.sync.dma_start(out=raw[:], in_=w_rows[:, :, lo:hi])
             w_raw.append(raw)
@@ -73,24 +77,13 @@ def tile_picked_lnfold_none_po_kernel(
         nc.gpsimd.memset(signs[:, 0, :], -1.0)
         nc.gpsimd.memset(signs[:, 1, :], 1.0)
 
-        stats_g = sb.tile([P, S], F32, name="stats_g", tag="picked", align_bytes=64)
-        nc.vector.tensor_copy(stats_g[:], stats[:].indirect(offsets[:]))
-        xw = sb.tile([P, S], U32, name="xw", align_bytes=64)
-        nc.vector.tensor_copy(xw[:], xw_all[:].indirect(offsets[:]))
+        stats_g = reuse.tile([P, S], F32, name="stats_g", offset=0, align_bytes=64)
+        for h in range(2):
+            nc.vector.tensor_copy(stats_g[:, h * HALF : (h + 1) * HALF], stats[:].indirect(half_offsets[h]))
+        xw_a = sb.tile([P, HALF], U32, name="xw_a", align_bytes=64)
+        nc.vector.tensor_copy(xw_a[:], xw_all[:].indirect(half_offsets[0]))
 
-        w_bf = sb.tile([P, PACK, P, PACK], BF16, name="w_bf", align_bytes=64)
-
-        def cast_w(part):
-            lo, hi = W_PARTS[part]
-            nc.scalar.activation(
-                out=w_bf[:, :, lo // PACK : hi // PACK, :].rearrange("p t m j -> p m j t"),
-                in_=w_raw[part][:].rearrange("p j (m t) -> p m j t", t=PACK),
-                func=ACT.Copy,
-            )
-
-        cast_w(0)
-
-        turned = ps.tile([P, CHUNKS, P], F32, name="turned")
+        turned = ps.tile([P, CHUNKS, P], F32, name="turned", tag="turn")
         for c in range(CHUNKS):
             nc.tensor.transpose(turned[:, c, :], stats_g[:, c * CHUNK : (c + 1) * CHUNK], ident[:])
         stat_cols = sb.tile([P, 2, CHUNKS], F32, name="stat_cols")
@@ -104,12 +97,14 @@ def tile_picked_lnfold_none_po_kernel(
         shift_col = sb.tile([P, CHUNKS], F32, name="shift_col")
         nc.gpsimd.tensor_tensor(out=shift_col[:], in0=stat_cols[:, 0, :], in1=inv_col, op=ALU.mult)
 
-        xs = sb.tile([P, S], U8, name="xs", tag="picked", align_bytes=64)
-        nc.vector.tensor_copy(xs[:], xs_all[:].indirect(offsets[:]))
+        xw_b = reuse.tile([P, HALF], U32, name="xw_b", offset=0, align_bytes=64)
+        nc.vector.tensor_copy(xw_b[:], xw_all[:].indirect(half_offsets[1]))
+        xs_a = reuse.tile([P, HALF], U8, name="xs_a", offset=4 * HALF, align_bytes=64)
+        nc.vector.tensor_copy(xs_a[:], xs_all[:].indirect(half_offsets[0]))
 
-        inv_ps = ps.tile([P, S], F32, name="inv_ps")
+        inv_ps = ps.tile([P, HALF], F32, name="inv_ps")
         shift_ps = ps.tile([P, S], F32, name="shift_ps")
-        for c in range(CHUNKS):
+        for c in range(DIRECT):
             nc.tensor.transpose(
                 inv_ps[:, c * CHUNK : (c + 1) * CHUNK], inv_col[:, c : c + 1].to_broadcast([P, P]), ident[:]
             )
@@ -118,31 +113,53 @@ def tile_picked_lnfold_none_po_kernel(
                 shift_ps[:, c * CHUNK : (c + 1) * CHUNK], shift_col[:, c : c + 1].to_broadcast([P, P]), ident[:]
             )
 
-        for part in range(1, len(W_PARTS)):
-            cast_w(part)
+        w_bf = sb.tile([P, PACK, P, PACK], BF16, name="w_bf", align_bytes=64)
+        for part, (lo, hi) in enumerate(W_PARTS):
+            dst = w_bf[:, :, lo // PACK : hi // PACK, :].rearrange("p t m j -> p m j t")
+            src = w_raw[part][:].rearrange("p j (m t) -> p m j t", t=PACK)
+            if part < len(W_PARTS) - 1:
+                nc.scalar.activation(out=dst, in_=src, func=ACT.Copy)
+            else:
+                nc.vector.tensor_copy(out=dst, in_=src)
 
         w_codes = sb.tile([P, N], U32, name="w_codes", align_bytes=64)
-        w_scales = sb.tile([P, N], U8, name="w_scales", tag="scales_in", align_bytes=64)
+        w_scales = sb.tile([P, N], U8, name="w_scales", align_bytes=64)
         for t in range(PACK):
             nc.vector.quantize_mx(
                 out=w_codes[:, t * P : (t + 1) * P].bitcast(FP8X4),
                 scales=w_scales[:, t * P : (t + 1) * P],
                 in_=w_bf[:, t, :, :].rearrange("p m j -> p (m j)"),
             )
+        xs_b = sb.tile([P, HALF], U8, name="xs_b", tag="w_raw%d" % (len(W_PARTS) - 1), align_bytes=64)
+        nc.vector.tensor_copy(xs_b[:], xs_all[:].indirect(half_offsets[1]))
 
-        inv_rows = sb.tile([P, S], F32, name="inv_rows", align_bytes=64)
-        nc.vector.tensor_copy(out=inv_rows[:], in_=inv_ps[:])
+        inv_rows = sb.tile([P, HALF], F32, name="inv_rows", align_bytes=64)
+        nc.scalar.copy(out=inv_rows[:], in_=inv_ps[:])
+
+        addends = []
+
+        def make_addend(h):
+            addend = sb.tile([P, PACK, HALF], F32, name="addend%d" % h, align_bytes=64)
+            for t in range(PACK):
+                nc.scalar.activation(
+                    out=addend[:, t, :],
+                    in_=shift_ps[:, h * HALF : (h + 1) * HALF],
+                    func=ACT.Identity,
+                    scale=g_cols[:, t : t + 1],
+                    bias=b_cols[:, t : t + 1],
+                )
+            addends.append(addend)
 
         y_codes = sb.tile([P, S], U32, name="y_codes", align_bytes=64)
         y_scales = sb.tile([P, S], U8, name="y_scales", align_bytes=64)
         out_rows = out_0.rearrange("(p t) j -> p t j", t=PACK)
         out_words = out_1[0].rearrange("p c r -> p (c r)").bitcast(I32)
 
+        scaled = []
         results = []
-        addends = []
-        scaleds = []
+        roundeds = []
 
-        def product(c):
+        def scale_direct(c):
             cols = slice(c * CHUNK, (c + 1) * CHUNK)
             acc = ps.tile([P, PACK, CHUNK], F32, name="acc%d" % c)
             for t in range(PACK):
@@ -150,68 +167,91 @@ def tile_picked_lnfold_none_po_kernel(
                     out=acc[:, t, :],
                     lhsT=w_codes[:, t * P : (t + 1) * P].bitcast(FP8X4),
                     lhsT_scale=w_scales[:, t * P : (t + 1) * P],
-                    rhs=xw[:, cols].bitcast(FP8X4),
-                    rhs_scale=xs[:, cols],
+                    rhs=xw_a[:, cols].bitcast(FP8X4),
+                    rhs_scale=xs_a[:, cols],
                     start=True,
                     stop=True,
                 )
-            addend = sb.tile([P, PACK, CHUNK], F32, name="addend%d" % c, align_bytes=64)
-            for t in range(PACK):
-                nc.scalar.activation(
-                    out=addend[:, t, :],
-                    in_=shift_ps[:, cols],
-                    func=ACT.Identity,
-                    scale=g_cols[:, t : t + 1],
-                    bias=b_cols[:, t : t + 1],
-                )
-            scaled = sb.tile([P, PACK, CHUNK], F32, name="scaled%d" % c, align_bytes=64)
+            z = sb.tile([P, PACK, CHUNK], F32, name="scaled%d" % c, align_bytes=64)
             nc.vector.tensor_tensor(
-                out=scaled[:],
+                out=z[:],
                 in0=acc[:],
                 in1=inv_rows[:, cols].unsqueeze(1).to_broadcast([P, PACK, CHUNK]),
                 op=ALU.mult,
             )
-            addends.append(addend)
-            scaleds.append(scaled)
+            scaled.append(z)
+
+        by_token = []
+
+        def scale_turned(c):
+            cols = slice(c * CHUNK - HALF, (c + 1) * CHUNK - HALF)
+            acc = ps.tile([P, N], F32, name="acc%d" % c)
+            nc.tensor.matmul_mx(
+                out=acc[:],
+                lhsT=xw_b[:, cols].bitcast(FP8X4),
+                lhsT_scale=xs_b[:, cols],
+                rhs=w_codes[:].bitcast(FP8X4),
+                rhs_scale=w_scales[:],
+                start=True,
+                stop=True,
+            )
+            z = sb.tile([P, N], F32, name="by_token%d" % c, align_bytes=64)
+            nc.scalar.activation(out=z[:], in_=acc[:], func=ACT.Copy, scale=inv_col[:, c : c + 1])
+            by_token.append(z)
+
+        def turn_back(c):
+            back = ps.tile([P, PACK, CHUNK], F32, name="back%d" % c, tag="turn" if c == DIRECT else "back")
+            for t in range(PACK):
+                nc.tensor.transpose(back[:, t, :], by_token[c - DIRECT][:, t * P : (t + 1) * P], ident[:])
+            scaled.append(back)
 
         def finish(c):
             cols = slice(c * CHUNK, (c + 1) * CHUNK)
+            in_half = slice(c * CHUNK % HALF, c * CHUNK % HALF + CHUNK)
             result = sb.tile([P, PACK, CHUNK], F32, name="result%d" % c, align_bytes=64)
-            nc.vector.tensor_tensor(out=result[:], in0=scaleds[c][:], in1=addends[c][:], op=ALU.add)
+            nc.vector.tensor_tensor(
+                out=result[:], in0=scaled[c][:], in1=addends[c // DIRECT][:, :, in_half], op=ALU.add
+            )
             nc.sync.dma_start(out=out_rows[:, :, cols], in_=result[:])
             results.append(result)
 
-        roundeds = []
-
-        def round_result(c):
+        def round_result(c, engine_copy):
             rounded = sb.tile([P, CHUNK, PACK], BF16, name="rounded%d" % c, align_bytes=64)
-            dst = rounded[:].rearrange("p (c i) t -> p c t i", i=4)
-            src = results[c][:].rearrange("p t (c i) -> p c t i", i=4)
-            if c == CHUNKS - 1:
-                nc.vector.tensor_copy(out=dst, in_=src)
-            else:
-                nc.scalar.copy(out=dst, in_=src)
+            engine_copy(
+                out=rounded[:].rearrange("p (c i) t -> p c t i", i=4),
+                in_=results[c][:].rearrange("p t (c i) -> p c t i", i=4),
+            )
             roundeds.append(rounded)
 
         def planes(c):
             cols = slice(c * CHUNK, (c + 1) * CHUNK)
-            rounded = roundeds[c]
             nc.vector.quantize_mx(
                 out=y_codes[:, cols].bitcast(FP8X4),
                 scales=y_scales[:, cols],
-                in_=rounded[:].rearrange("p c t -> p (c t)"),
+                in_=roundeds[c][:].rearrange("p c t -> p (c t)"),
             )
             nc.sync.dma_start(out=out_words[:, cols], in_=y_codes[:, cols].bitcast(I32))
 
-        for step in range(CHUNKS + 2):
-            if step < CHUNKS:
-                product(step)
-            if 0 <= step - 1 < CHUNKS:
-                finish(step - 1)
-            if 0 <= step - 2 < CHUNKS:
-                planes(step - 2)
-            if 0 <= step - 1 < CHUNKS:
-                round_result(step - 1)
+        make_addend(0)
+        for c in range(DIRECT):
+            scale_direct(c)
+        for c in range(DIRECT, CHUNKS):
+            scale_turned(c)
+        make_addend(1)
+        for c in range(DIRECT, CHUNKS):
+            turn_back(c)
+        finish(0)
+        finish(1)
+        round_result(0, nc.vector.tensor_copy)
+        round_result(1, nc.vector.tensor_copy)
+        finish(2)
+        finish(3)
+        round_result(2, nc.scalar.copy)
+        planes(0)
+        planes(1)
+        round_result(3, nc.vector.tensor_copy)
+        planes(2)
+        planes(3)
         for q in range(4):
             queue = nc.sync if q % 2 == 0 else nc.scalar
             queue.dma_start(

@@ -20,7 +20,7 @@ CHUNK = 128
 CHUNKS = S // CHUNK
 HALF = S // 2
 DIRECT = CHUNKS // 2
-W_PARTS = ((0, 192), (192, 384), (384, 512))
+W_PARTS = ((0, 256), (256, 512))
 MEAN_ROW, INV_ROW = 96, 112
 FLOPS = 2 * K * S * N
 BYTES = 4 * P * T + 16 * T + 2 * 4 * T + 2 * 4 * N + 4 * K * N + 2 * S * 8 + 4 * N * S + N * S + 16 * S
@@ -47,35 +47,42 @@ def tile_picked_lnfold_none_po_kernel(
         nc.vector.memset(xs_all[:].bitcast(I32), 0)
         nc.vector.memset(stats[0:MEAN_ROW, :], 0.0)
 
-        xw_all = sb.tile([P, T], U32, name="xw_all", align_bytes=64)
+        xw_all = reuse.tile([P, T], U32, name="xw_all", offset=4 * S, align_bytes=64)
         nc.sync.dma_start(
             out=xw_all[:].bitcast(I32),
             in_=x_words[0].rearrange("p c r -> p (c r)").bitcast(I32),
         )
 
+
+        def load_scales(queue, q):
+            queue.dma_start(
+                out=xs_all[32 * q : 32 * q + 4, :].bitcast(I32),
+                in_=x_scales[0][4 * q : 4 * q + 4, :].bitcast(I32),
+            )
+
+        load_scales(nc.scalar, 0)
+        load_scales(nc.scalar, 1)
+
         w_rows = w1.rearrange("(p j) c -> p j c", j=PACK)
         w_raw = []
         for part, (lo, hi) in enumerate(W_PARTS):
-            if part == len(W_PARTS) - 1:
-                for q in range(4):
-                    nc.sync.dma_start(
-                        out=xs_all[32 * q : 32 * q + 4, :].bitcast(I32),
-                        in_=x_scales[0][4 * q : 4 * q + 4, :].bitcast(I32),
-                    )
             raw = sb.tile([P, PACK, hi - lo], F32, name="w_raw%d" % part, align_bytes=64)
             nc.sync.dma_start(out=raw[:], in_=w_rows[:, :, lo:hi])
             w_raw.append(raw)
+            if part == 0:
+                load_scales(nc.sync, 2)
+                load_scales(nc.sync, 3)
+
+        ident = sb.tile([P, P], F32, name="ident", align_bytes=64)
+        make_identity(nc, ident[:])
+        signs = sb.tile([P, 2, CHUNKS], F32, name="signs")
+        nc.vector.memset(signs[:, 0, :], -1.0)
+        nc.vector.memset(signs[:, 1, :], 1.0)
 
         g_cols = sb.tile([P, PACK], F32, name="g_cols")
         b_cols = sb.tile([P, PACK], F32, name="b_cols")
         nc.sync.dma_start(out=g_cols[:], in_=gsum.rearrange("(p t) o -> p (t o)", t=PACK))
         nc.sync.dma_start(out=b_cols[:], in_=b.rearrange("(p t) o -> p (t o)", t=PACK))
-
-        ident = sb.tile([P, P], F32, name="ident", align_bytes=64)
-        make_identity(nc, ident[:])
-        signs = sb.tile([P, 2, CHUNKS], F32, name="signs")
-        nc.gpsimd.memset(signs[:, 0, :], -1.0)
-        nc.gpsimd.memset(signs[:, 1, :], 1.0)
 
         stats_g = reuse.tile([P, S], F32, name="stats_g", offset=0, align_bytes=64)
         for h in range(2):
@@ -113,23 +120,36 @@ def tile_picked_lnfold_none_po_kernel(
                 shift_ps[:, c * CHUNK : (c + 1) * CHUNK], shift_col[:, c : c + 1].to_broadcast([P, P]), ident[:]
             )
 
-        w_bf = sb.tile([P, PACK, P, PACK], BF16, name="w_bf", align_bytes=64)
-        for part, (lo, hi) in enumerate(W_PARTS):
-            dst = w_bf[:, :, lo // PACK : hi // PACK, :].rearrange("p t m j -> p m j t")
+        w_bf = [
+            sb.tile([P, PACK, P // 2, PACK], BF16, name="w_bf0", align_bytes=64),
+            reuse.tile([P, PACK, P // 2, PACK], BF16, name="w_bf1", offset=4 * S, align_bytes=64),
+        ]
+        w_codes = reuse.tile([P, N], U32, name="w_codes", offset=4 * S + 2 * T, align_bytes=64)
+        w_scales = sb.tile([P, N], U8, name="w_scales", align_bytes=64)
+
+        def cast_w(part):
+            lo, hi = W_PARTS[part]
+            first = lo % (N // 2) // PACK
+            dst = w_bf[lo // (N // 2)][:, :, first : first + (hi - lo) // PACK, :].rearrange("p t m j -> p m j t")
             src = w_raw[part][:].rearrange("p j (m t) -> p m j t", t=PACK)
             if part < len(W_PARTS) - 1:
                 nc.scalar.activation(out=dst, in_=src, func=ACT.Copy)
             else:
                 nc.vector.tensor_copy(out=dst, in_=src)
 
-        w_codes = sb.tile([P, N], U32, name="w_codes", align_bytes=64)
-        w_scales = sb.tile([P, N], U8, name="w_scales", align_bytes=64)
-        for t in range(PACK):
-            nc.vector.quantize_mx(
-                out=w_codes[:, t * P : (t + 1) * P].bitcast(FP8X4),
-                scales=w_scales[:, t * P : (t + 1) * P],
-                in_=w_bf[:, t, :, :].rearrange("p m j -> p (m j)"),
-            )
+        def quantize_w(h):
+            for t in range(PACK):
+                cols = slice(t * P + h * P // 2, t * P + (h + 1) * P // 2)
+                nc.vector.quantize_mx(
+                    out=w_codes[:, cols].bitcast(FP8X4),
+                    scales=w_scales[:, cols],
+                    in_=w_bf[h][:, t, :, :].rearrange("p m j -> p (m j)"),
+                )
+
+        cast_w(0)
+        quantize_w(0)
+        cast_w(1)
+        quantize_w(1)
         xs_b = sb.tile([P, HALF], U8, name="xs_b", tag="w_raw%d" % (len(W_PARTS) - 1), align_bytes=64)
         nc.vector.tensor_copy(xs_b[:], xs_all[:].indirect(half_offsets[1]))
 
@@ -155,31 +175,40 @@ def tile_picked_lnfold_none_po_kernel(
         out_rows = out_0.rearrange("(p t) j -> p t j", t=PACK)
         out_words = out_1[0].rearrange("p c r -> p (c r)").bitcast(I32)
 
-        scaled = []
-        results = []
+        result_a = sb.tile([P, PACK, HALF], F32, name="result_a", align_bytes=64)
+        scaled_a = []
+        backs = []
+        results = [result_a[:, :, c * CHUNK : (c + 1) * CHUNK] for c in range(DIRECT)]
         roundeds = []
 
-        def scale_direct(c):
-            cols = slice(c * CHUNK, (c + 1) * CHUNK)
-            acc = ps.tile([P, PACK, CHUNK], F32, name="acc%d" % c)
-            for t in range(PACK):
+        def scale_direct(u):
+            acc = ps.tile([P, 2, HALF], F32, name="acc%d" % u)
+            for i in range(2):
+                t = 2 * u + i
                 nc.tensor.matmul_mx(
-                    out=acc[:, t, :],
+                    out=acc[:, i, :],
                     lhsT=w_codes[:, t * P : (t + 1) * P].bitcast(FP8X4),
                     lhsT_scale=w_scales[:, t * P : (t + 1) * P],
-                    rhs=xw_a[:, cols].bitcast(FP8X4),
-                    rhs_scale=xs_a[:, cols],
+                    rhs=xw_a[:].bitcast(FP8X4),
+                    rhs_scale=xs_a[:],
                     start=True,
                     stop=True,
                 )
-            z = sb.tile([P, PACK, CHUNK], F32, name="scaled%d" % c, align_bytes=64)
+            z = sb.tile([P, 2, HALF], F32, name="scaled%d" % u, align_bytes=64)
             nc.vector.tensor_tensor(
                 out=z[:],
                 in0=acc[:],
-                in1=inv_rows[:, cols].unsqueeze(1).to_broadcast([P, PACK, CHUNK]),
+                in1=inv_rows[:].unsqueeze(1).to_broadcast([P, 2, HALF]),
                 op=ALU.mult,
             )
-            scaled.append(z)
+            scaled_a.append(z)
+
+        def finish_direct(u):
+            pair = slice(2 * u, 2 * u + 2)
+            nc.vector.tensor_tensor(
+                out=result_a[:, pair, :], in0=scaled_a[u][:], in1=addends[0][:, pair, :], op=ALU.add
+            )
+            nc.sync.dma_start(out=out_rows[:, pair, 0:HALF], in_=result_a[:, pair, :])
 
         by_token = []
 
@@ -203,23 +232,23 @@ def tile_picked_lnfold_none_po_kernel(
             back = ps.tile([P, PACK, CHUNK], F32, name="back%d" % c, tag="turn" if c == DIRECT else "back")
             for t in range(PACK):
                 nc.tensor.transpose(back[:, t, :], by_token[c - DIRECT][:, t * P : (t + 1) * P], ident[:])
-            scaled.append(back)
+            backs.append(back)
 
-        def finish(c):
+        def finish_turned(c):
             cols = slice(c * CHUNK, (c + 1) * CHUNK)
-            in_half = slice(c * CHUNK % HALF, c * CHUNK % HALF + CHUNK)
+            in_half = slice(c * CHUNK - HALF, (c + 1) * CHUNK - HALF)
             result = sb.tile([P, PACK, CHUNK], F32, name="result%d" % c, align_bytes=64)
             nc.vector.tensor_tensor(
-                out=result[:], in0=scaled[c][:], in1=addends[c // DIRECT][:, :, in_half], op=ALU.add
+                out=result[:], in0=backs[c - DIRECT][:], in1=addends[1][:, :, in_half], op=ALU.add
             )
             nc.sync.dma_start(out=out_rows[:, :, cols], in_=result[:])
-            results.append(result)
+            results.append(result[:])
 
         def round_result(c, engine_copy):
             rounded = sb.tile([P, CHUNK, PACK], BF16, name="rounded%d" % c, align_bytes=64)
             engine_copy(
                 out=rounded[:].rearrange("p (c i) t -> p c t i", i=4),
-                in_=results[c][:].rearrange("p t (c i) -> p c t i", i=4),
+                in_=results[c].rearrange("p t (c i) -> p c t i", i=4),
             )
             roundeds.append(rounded)
 
@@ -230,28 +259,32 @@ def tile_picked_lnfold_none_po_kernel(
                 scales=y_scales[:, cols],
                 in_=roundeds[c][:].rearrange("p c t -> p (c t)"),
             )
-            nc.sync.dma_start(out=out_words[:, cols], in_=y_codes[:, cols].bitcast(I32))
+
+        def store_words(queue, lo, hi):
+            queue.dma_start(out=out_words[:, lo:hi], in_=y_codes[:, lo:hi].bitcast(I32))
 
         make_addend(0)
-        for c in range(DIRECT):
-            scale_direct(c)
+        for u in range(2):
+            scale_direct(u)
         for c in range(DIRECT, CHUNKS):
             scale_turned(c)
         make_addend(1)
         for c in range(DIRECT, CHUNKS):
             turn_back(c)
-        finish(0)
-        finish(1)
-        round_result(0, nc.vector.tensor_copy)
-        round_result(1, nc.vector.tensor_copy)
-        finish(2)
-        finish(3)
-        round_result(2, nc.scalar.copy)
+        for u in range(2):
+            finish_direct(u)
+        for c in range(DIRECT, CHUNKS):
+            finish_turned(c)
+        for c in range(CHUNKS - 1):
+            round_result(c, nc.scalar.copy)
         planes(0)
         planes(1)
-        round_result(3, nc.vector.tensor_copy)
+        round_result(CHUNKS - 1, nc.vector.tensor_copy)
         planes(2)
         planes(3)
+        store_words(nc.sync, 0, HALF)
+        store_words(nc.sync, HALF, S - CHUNK)
+        store_words(nc.scalar, S - CHUNK, S)
         for q in range(4):
             queue = nc.sync if q % 2 == 0 else nc.scalar
             queue.dma_start(

@@ -20,8 +20,8 @@ CHUNK = 128
 CHUNKS = S // CHUNK
 HALF = S // 2
 DIRECT = CHUNKS // 2
-W_PARTS = ((0, 256), (256, 512))
-MEAN_ROW, INV_ROW = 96, 112
+W_PARTS = ((0, 256), (256, 384), (384, 512))
+MEAN_ROW, INV_ROW = 126, 127
 FLOPS = 2 * K * S * N
 BYTES = 4 * P * T + 16 * T + 2 * 4 * T + 2 * 4 * N + 4 * K * N + 2 * S * 8 + 4 * N * S + N * S + 16 * S
 
@@ -40,8 +40,8 @@ def tile_picked_lnfold_none_po_kernel(
         half_offsets = [offsets[:, h * HALF // 16 : (h + 1) * HALF // 16] for h in range(2)]
 
         stats = sb.tile([P, T], F32, name="stats", align_bytes=64)
-        nc.sync.dma_start(out=stats[MEAN_ROW:INV_ROW, :], in_=mean[MEAN_ROW:INV_ROW, :])
-        nc.scalar.dma_start(out=stats[INV_ROW:P, :], in_=inv[INV_ROW:P, :])
+        nc.sync.dma_start(out=stats[MEAN_ROW:INV_ROW, :], in_=mean[0:1, :])
+        nc.scalar.dma_start(out=stats[INV_ROW:P, :], in_=inv[0:1, :])
 
         xs_all = sb.tile([P, T], U8, name="xs_all", align_bytes=64)
         nc.vector.memset(xs_all[:].bitcast(I32), 0)
@@ -96,7 +96,7 @@ def tile_picked_lnfold_none_po_kernel(
         stat_cols = sb.tile([P, 2, CHUNKS], F32, name="stat_cols")
         nc.vector.tensor_tensor(
             out=stat_cols[:],
-            in0=turned[:, :, MEAN_ROW : P : INV_ROW - MEAN_ROW].rearrange("p c s -> p s c"),
+            in0=turned[:, :, MEAN_ROW:P].rearrange("p c s -> p s c"),
             in1=signs[:],
             op=ALU.mult,
         )
@@ -122,9 +122,9 @@ def tile_picked_lnfold_none_po_kernel(
 
         w_bf = [
             sb.tile([P, PACK, P // 2, PACK], BF16, name="w_bf0", align_bytes=64),
-            reuse.tile([P, PACK, P // 2, PACK], BF16, name="w_bf1", offset=4 * S, align_bytes=64),
+            reuse.tile([P, PACK, P // 2, PACK], BF16, name="w_bf1", offset=4 * S + 2 * T, align_bytes=64),
         ]
-        w_codes = reuse.tile([P, N], U32, name="w_codes", offset=4 * S + 2 * T, align_bytes=64)
+        w_codes = reuse.tile([P, N], U32, name="w_codes", offset=4 * S, align_bytes=64)
         w_scales = sb.tile([P, N], U8, name="w_scales", align_bytes=64)
 
         def cast_w(part):
@@ -147,8 +147,9 @@ def tile_picked_lnfold_none_po_kernel(
                 )
 
         cast_w(0)
-        quantize_w(0)
         cast_w(1)
+        quantize_w(0)
+        cast_w(2)
         quantize_w(1)
         xs_b = sb.tile([P, HALF], U8, name="xs_b", tag="w_raw%d" % (len(W_PARTS) - 1), align_bytes=64)
         nc.vector.tensor_copy(xs_b[:], xs_all[:].indirect(half_offsets[1]))
@@ -156,19 +157,33 @@ def tile_picked_lnfold_none_po_kernel(
         inv_rows = sb.tile([P, HALF], F32, name="inv_rows", align_bytes=64)
         nc.scalar.copy(out=inv_rows[:], in_=inv_ps[:])
 
-        addends = []
+        shift_rows = sb.tile([P, HALF], F32, name="shift_rows", align_bytes=64)
+        nc.scalar.copy(out=shift_rows[:], in_=shift_ps[:, HALF:S])
+
+        addends = [
+            sb.tile([P, PACK, HALF], F32, name="addend0", align_bytes=64),
+            reuse.tile([P, PACK, HALF], F32, name="addend1", offset=4 * S + 2 * T, align_bytes=64),
+        ]
 
         def make_addend(h):
-            addend = sb.tile([P, PACK, HALF], F32, name="addend%d" % h, align_bytes=64)
             for t in range(PACK):
-                nc.scalar.activation(
-                    out=addend[:, t, :],
-                    in_=shift_ps[:, h * HALF : (h + 1) * HALF],
-                    func=ACT.Identity,
-                    scale=g_cols[:, t : t + 1],
-                    bias=b_cols[:, t : t + 1],
-                )
-            addends.append(addend)
+                if h == 0:
+                    nc.scalar.activation(
+                        out=addends[0][:, t, :],
+                        in_=shift_ps[:, 0:HALF],
+                        func=ACT.Identity,
+                        scale=g_cols[:, t : t + 1],
+                        bias=b_cols[:, t : t + 1],
+                    )
+                else:
+                    nc.gpsimd.tensor_scalar(
+                        out=addends[1][:, t, :],
+                        in0=shift_rows[:],
+                        scalar1=g_cols[:, t : t + 1],
+                        scalar2=b_cols[:, t : t + 1],
+                        op0=ALU.mult,
+                        op1=ALU.add,
+                    )
 
         y_codes = sb.tile([P, S], U32, name="y_codes", align_bytes=64)
         y_scales = sb.tile([P, S], U8, name="y_scales", align_bytes=64)
@@ -282,8 +297,7 @@ def tile_picked_lnfold_none_po_kernel(
         round_result(CHUNKS - 1, nc.vector.tensor_copy)
         planes(2)
         planes(3)
-        store_words(nc.sync, 0, HALF)
-        store_words(nc.sync, HALF, S - CHUNK)
+        store_words(nc.sync, 0, S - CHUNK)
         store_words(nc.scalar, S - CHUNK, S)
         for q in range(4):
             queue = nc.sync if q % 2 == 0 else nc.scalar

@@ -44,7 +44,7 @@ def tile_picked_lnfold_none_po_kernel(
         nc.scalar.dma_start(out=stats[INV_ROW:P, :], in_=inv[0:1, :])
 
         xs_all = sb.tile([P, T], U8, name="xs_all", align_bytes=64)
-        nc.vector.memset(xs_all[:].bitcast(I32), 0)
+        nc.gpsimd.memset(xs_all[:].bitcast(I32), 0)
         nc.vector.memset(stats[0:MEAN_ROW, :], 0.0)
 
         xw_all = reuse.tile([P, T], U32, name="xw_all", offset=4 * S, align_bytes=64)
@@ -109,7 +109,7 @@ def tile_picked_lnfold_none_po_kernel(
         xs_a = reuse.tile([P, HALF], U8, name="xs_a", offset=4 * HALF, align_bytes=64)
         nc.vector.tensor_copy(xs_a[:], xs_all[:].indirect(half_offsets[0]))
 
-        inv_ps = ps.tile([P, HALF], F32, name="inv_ps")
+        inv_ps = ps.tile([P, HALF], F32, name="inv_ps", tag="inv")
         shift_ps = ps.tile([P, S], F32, name="shift_ps")
         for c in range(DIRECT):
             nc.tensor.transpose(
@@ -148,10 +148,10 @@ def tile_picked_lnfold_none_po_kernel(
 
         cast_w(0)
         cast_w(1)
-        quantize_w(0)
         cast_w(2)
+        quantize_w(0)
         quantize_w(1)
-        xs_b = sb.tile([P, HALF], U8, name="xs_b", tag="w_raw%d" % (len(W_PARTS) - 1), align_bytes=64)
+        xs_b = reuse.tile([P, HALF], U8, name="xs_b", offset=4 * S + 2 * T, align_bytes=64)
         nc.vector.tensor_copy(xs_b[:], xs_all[:].indirect(half_offsets[1]))
 
         inv_rows = sb.tile([P, HALF], F32, name="inv_rows", align_bytes=64)
@@ -162,15 +162,15 @@ def tile_picked_lnfold_none_po_kernel(
 
         addends = [
             sb.tile([P, PACK, HALF], F32, name="addend0", align_bytes=64),
-            reuse.tile([P, PACK, HALF], F32, name="addend1", offset=4 * S + 2 * T, align_bytes=64),
+            reuse.tile([P, PACK, HALF], F32, name="addend1", offset=4 * S + 2 * T + HALF, align_bytes=64),
         ]
 
         def make_addend(h):
             for t in range(PACK):
-                if h == 0:
+                if h == 0 or t == PACK - 1:
                     nc.scalar.activation(
-                        out=addends[0][:, t, :],
-                        in_=shift_ps[:, 0:HALF],
+                        out=addends[h][:, t, :],
+                        in_=shift_ps[:, h * HALF : (h + 1) * HALF],
                         func=ACT.Identity,
                         scale=g_cols[:, t : t + 1],
                         bias=b_cols[:, t : t + 1],
@@ -197,7 +197,7 @@ def tile_picked_lnfold_none_po_kernel(
         roundeds = []
 
         def scale_direct(u):
-            acc = ps.tile([P, 2, HALF], F32, name="acc%d" % u)
+            acc = ps.tile([P, 2, HALF], F32, name="acc%d" % u, tag="acc%d" % u)
             for i in range(2):
                 t = 2 * u + i
                 nc.tensor.matmul_mx(
@@ -240,22 +240,32 @@ def tile_picked_lnfold_none_po_kernel(
                 stop=True,
             )
             z = sb.tile([P, N], F32, name="by_token%d" % c, align_bytes=64)
-            nc.scalar.activation(out=z[:], in_=acc[:], func=ACT.Copy, scale=inv_col[:, c : c + 1])
+            for u in range(2):
+                pair = slice(u * N // 2, (u + 1) * N // 2)
+                nc.scalar.activation(out=z[:, pair], in_=acc[:, pair], func=ACT.Copy, scale=inv_col[:, c : c + 1])
             by_token.append(z)
 
         def turn_back(c):
-            back = ps.tile([P, PACK, CHUNK], F32, name="back%d" % c, tag="turn" if c == DIRECT else "back")
-            for t in range(PACK):
-                nc.tensor.transpose(back[:, t, :], by_token[c - DIRECT][:, t * P : (t + 1) * P], ident[:])
-            backs.append(back)
+            for u in range(2):
+                tag = ("turn", "inv", "back", "acc0")[2 * (c - DIRECT) + u]
+                back = ps.tile([P, 2, CHUNK], F32, name="back%d%d" % (c, u), tag=tag)
+                for i in range(2):
+                    t = 2 * u + i
+                    nc.tensor.transpose(back[:, i, :], by_token[c - DIRECT][:, t * P : (t + 1) * P], ident[:])
+                backs.append(back)
 
         def finish_turned(c):
             cols = slice(c * CHUNK, (c + 1) * CHUNK)
             in_half = slice(c * CHUNK - HALF, (c + 1) * CHUNK - HALF)
             result = sb.tile([P, PACK, CHUNK], F32, name="result%d" % c, align_bytes=64)
-            nc.vector.tensor_tensor(
-                out=result[:], in0=backs[c - DIRECT][:], in1=addends[1][:, :, in_half], op=ALU.add
-            )
+            for u in range(2):
+                pair = slice(2 * u, 2 * u + 2)
+                nc.vector.tensor_tensor(
+                    out=result[:, pair, :],
+                    in0=backs[2 * (c - DIRECT) + u][:],
+                    in1=addends[1][:, pair, in_half],
+                    op=ALU.add,
+                )
             nc.sync.dma_start(out=out_rows[:, :, cols], in_=result[:])
             results.append(result[:])
 
@@ -279,11 +289,11 @@ def tile_picked_lnfold_none_po_kernel(
             queue.dma_start(out=out_words[:, lo:hi], in_=y_codes[:, lo:hi].bitcast(I32))
 
         make_addend(0)
+        make_addend(1)
         for u in range(2):
             scale_direct(u)
         for c in range(DIRECT, CHUNKS):
             scale_turned(c)
-        make_addend(1)
         for c in range(DIRECT, CHUNKS):
             turn_back(c)
         for u in range(2):

@@ -20,7 +20,10 @@ CHUNK = 128
 CHUNKS = S // CHUNK
 HALF = S // 2
 DIRECT = CHUNKS // 2
-W_PARTS = ((0, 256), (256, 384), (384, 512))
+W_BF1 = 3 * HALF
+W_RAW = 8 * N
+XS_ALL = W_RAW + 16 * N
+GPSIMD_ROWS = 2
 MEAN_ROW, INV_ROW = 126, 127
 FLOPS = 2 * K * S * N
 BYTES = 4 * P * T + 16 * T + 2 * 4 * T + 2 * 4 * N + 4 * K * N + 2 * S * 8 + 4 * N * S + N * S + 16 * S
@@ -43,11 +46,11 @@ def tile_picked_lnfold_none_po_kernel(
         nc.sync.dma_start(out=stats[MEAN_ROW:INV_ROW, :], in_=mean[0:1, :])
         nc.scalar.dma_start(out=stats[INV_ROW:P, :], in_=inv[0:1, :])
 
-        xs_all = sb.tile([P, T], U8, name="xs_all", align_bytes=64)
+        xs_all = reuse.tile([P, T], U8, name="xs_all", offset=XS_ALL, align_bytes=64)
         nc.gpsimd.memset(xs_all[:].bitcast(I32), 0)
         nc.vector.memset(stats[0:MEAN_ROW, :], 0.0)
 
-        xw_all = reuse.tile([P, T], U32, name="xw_all", offset=4 * S, align_bytes=64)
+        xw_all = sb.tile([P, T], U32, name="xw_all", align_bytes=64)
         nc.sync.dma_start(
             out=xw_all[:].bitcast(I32),
             in_=x_words[0].rearrange("p c r -> p (c r)").bitcast(I32),
@@ -65,11 +68,11 @@ def tile_picked_lnfold_none_po_kernel(
 
         w_rows = w1.rearrange("(p j) c -> p j c", j=PACK)
         w_raw = []
-        for part, (lo, hi) in enumerate(W_PARTS):
-            raw = sb.tile([P, PACK, hi - lo], F32, name="w_raw%d" % part, align_bytes=64)
-            nc.sync.dma_start(out=raw[:], in_=w_rows[:, :, lo:hi])
+        for h in range(2):
+            raw = reuse.tile([P, PACK, N // 2], F32, name="w_raw%d" % h, offset=W_RAW + 8 * N * h, align_bytes=64)
+            nc.sync.dma_start(out=raw[:], in_=w_rows[:, :, h * N // 2 : (h + 1) * N // 2])
             w_raw.append(raw)
-            if part == 0:
+            if h == 0:
                 load_scales(nc.sync, 2)
                 load_scales(nc.sync, 3)
 
@@ -87,8 +90,9 @@ def tile_picked_lnfold_none_po_kernel(
         stats_g = reuse.tile([P, S], F32, name="stats_g", offset=0, align_bytes=64)
         for h in range(2):
             nc.vector.tensor_copy(stats_g[:, h * HALF : (h + 1) * HALF], stats[:].indirect(half_offsets[h]))
-        xw_a = sb.tile([P, HALF], U32, name="xw_a", align_bytes=64)
-        nc.vector.tensor_copy(xw_a[:], xw_all[:].indirect(half_offsets[0]))
+        xw_g = sb.tile([P, S], U32, name="xw_g", align_bytes=64)
+        nc.vector.tensor_copy(xw_g[:], xw_all[:].indirect(offsets[:]))
+        xw_a, xw_b = xw_g[:, 0:HALF], xw_g[:, HALF:S]
 
         turned = ps.tile([P, CHUNKS, P], F32, name="turned", tag="turn")
         for c in range(CHUNKS):
@@ -104,9 +108,7 @@ def tile_picked_lnfold_none_po_kernel(
         shift_col = sb.tile([P, CHUNKS], F32, name="shift_col")
         nc.gpsimd.tensor_tensor(out=shift_col[:], in0=stat_cols[:, 0, :], in1=inv_col, op=ALU.mult)
 
-        xw_b = reuse.tile([P, HALF], U32, name="xw_b", offset=0, align_bytes=64)
-        nc.vector.tensor_copy(xw_b[:], xw_all[:].indirect(half_offsets[1]))
-        xs_a = reuse.tile([P, HALF], U8, name="xs_a", offset=4 * HALF, align_bytes=64)
+        xs_a = reuse.tile([P, HALF], U8, name="xs_a", offset=0, align_bytes=64)
         nc.vector.tensor_copy(xs_a[:], xs_all[:].indirect(half_offsets[0]))
 
         inv_ps = ps.tile([P, HALF], F32, name="inv_ps", tag="inv")
@@ -122,20 +124,16 @@ def tile_picked_lnfold_none_po_kernel(
 
         w_bf = [
             sb.tile([P, PACK, P // 2, PACK], BF16, name="w_bf0", align_bytes=64),
-            reuse.tile([P, PACK, P // 2, PACK], BF16, name="w_bf1", offset=4 * S + 2 * T, align_bytes=64),
+            reuse.tile([P, PACK, P // 2, PACK], BF16, name="w_bf1", offset=W_BF1, align_bytes=64),
         ]
-        w_codes = reuse.tile([P, N], U32, name="w_codes", offset=4 * S, align_bytes=64)
-        w_scales = sb.tile([P, N], U8, name="w_scales", align_bytes=64)
+        w_codes = sb.tile([P, N], U32, name="w_codes", align_bytes=64)
+        w_scales = reuse.tile([P, N], U8, name="w_scales", offset=HALF, align_bytes=64)
 
-        def cast_w(part):
-            lo, hi = W_PARTS[part]
-            first = lo % (N // 2) // PACK
-            dst = w_bf[lo // (N // 2)][:, :, first : first + (hi - lo) // PACK, :].rearrange("p t m j -> p m j t")
-            src = w_raw[part][:].rearrange("p j (m t) -> p m j t", t=PACK)
-            if part < len(W_PARTS) - 1:
-                nc.scalar.activation(out=dst, in_=src, func=ACT.Copy)
-            else:
-                nc.vector.tensor_copy(out=dst, in_=src)
+        def cast_w(h, tiles, engine_copy):
+            engine_copy(
+                out=w_bf[h][:, tiles, :, :].rearrange("p t m j -> p m j t"),
+                in_=w_raw[h][:].rearrange("p j (m t) -> p m j t", t=PACK)[:, :, :, tiles],
+            )
 
         def quantize_w(h):
             for t in range(PACK):
@@ -146,28 +144,28 @@ def tile_picked_lnfold_none_po_kernel(
                     in_=w_bf[h][:, t, :, :].rearrange("p m j -> p (m j)"),
                 )
 
-        cast_w(0)
-        cast_w(1)
-        cast_w(2)
+        cast_w(0, slice(0, PACK), nc.scalar.copy)
+        cast_w(1, slice(2, PACK), nc.scalar.copy)
+        cast_w(1, slice(0, 2), nc.vector.tensor_copy)
         quantize_w(0)
         quantize_w(1)
-        xs_b = reuse.tile([P, HALF], U8, name="xs_b", offset=4 * S + 2 * T, align_bytes=64)
+        xs_b = reuse.tile([P, HALF], U8, name="xs_b", offset=W_RAW + 8 * N, align_bytes=64)
         nc.vector.tensor_copy(xs_b[:], xs_all[:].indirect(half_offsets[1]))
 
-        inv_rows = sb.tile([P, HALF], F32, name="inv_rows", align_bytes=64)
+        inv_rows = reuse.tile([P, HALF], F32, name="inv_rows", offset=W_RAW + 10 * N, align_bytes=64)
         nc.scalar.copy(out=inv_rows[:], in_=inv_ps[:])
 
-        shift_rows = sb.tile([P, HALF], F32, name="shift_rows", align_bytes=64)
+        shift_rows = reuse.tile([P, HALF], F32, name="shift_rows", offset=W_RAW + 12 * N, align_bytes=64)
         nc.scalar.copy(out=shift_rows[:], in_=shift_ps[:, HALF:S])
 
         addends = [
             sb.tile([P, PACK, HALF], F32, name="addend0", align_bytes=64),
-            reuse.tile([P, PACK, HALF], F32, name="addend1", offset=4 * S + 2 * T + HALF, align_bytes=64),
+            reuse.tile([P, PACK, HALF], F32, name="addend1", offset=XS_ALL, align_bytes=64),
         ]
 
         def make_addend(h):
             for t in range(PACK):
-                if h == 0 or t == PACK - 1:
+                if h == 0 or t >= GPSIMD_ROWS:
                     nc.scalar.activation(
                         out=addends[h][:, t, :],
                         in_=shift_ps[:, h * HALF : (h + 1) * HALF],
@@ -204,7 +202,7 @@ def tile_picked_lnfold_none_po_kernel(
                     out=acc[:, i, :],
                     lhsT=w_codes[:, t * P : (t + 1) * P].bitcast(FP8X4),
                     lhsT_scale=w_scales[:, t * P : (t + 1) * P],
-                    rhs=xw_a[:].bitcast(FP8X4),
+                    rhs=xw_a.bitcast(FP8X4),
                     rhs_scale=xs_a[:],
                     start=True,
                     stop=True,

@@ -22,8 +22,6 @@ HALF = S // 2
 DIRECT = CHUNKS // 2
 W_BF1 = 3 * HALF
 W_RAW = 8 * N
-XS_ALL = W_RAW + 16 * N
-GPSIMD_ROWS = 2
 MEAN_ROW, INV_ROW = 126, 127
 FLOPS = 2 * K * S * N
 BYTES = 4 * P * T + 16 * T + 2 * 4 * T + 2 * 4 * N + 4 * K * N + 2 * S * 8 + 4 * N * S + N * S + 16 * S
@@ -46,7 +44,7 @@ def tile_picked_lnfold_none_po_kernel(
         nc.sync.dma_start(out=stats[MEAN_ROW:INV_ROW, :], in_=mean[0:1, :])
         nc.scalar.dma_start(out=stats[INV_ROW:P, :], in_=inv[0:1, :])
 
-        xs_all = reuse.tile([P, T], U8, name="xs_all", offset=XS_ALL, align_bytes=64)
+        xs_all = sb.tile([P, T], U8, name="xs_all", align_bytes=64)
         nc.gpsimd.memset(xs_all[:].bitcast(I32), 0)
         nc.vector.memset(stats[0:MEAN_ROW, :], 0.0)
 
@@ -152,36 +150,23 @@ def tile_picked_lnfold_none_po_kernel(
         xs_b = reuse.tile([P, HALF], U8, name="xs_b", offset=W_RAW + 8 * N, align_bytes=64)
         nc.vector.tensor_copy(xs_b[:], xs_all[:].indirect(half_offsets[1]))
 
-        inv_rows = reuse.tile([P, HALF], F32, name="inv_rows", offset=W_RAW + 10 * N, align_bytes=64)
+        inv_rows = reuse.tile([P, HALF], F32, name="inv_rows", offset=W_RAW + 8 * N + HALF, align_bytes=64)
         nc.scalar.copy(out=inv_rows[:], in_=inv_ps[:])
 
-        shift_rows = reuse.tile([P, HALF], F32, name="shift_rows", offset=W_RAW + 12 * N, align_bytes=64)
-        nc.scalar.copy(out=shift_rows[:], in_=shift_ps[:, HALF:S])
-
         addends = [
-            sb.tile([P, PACK, HALF], F32, name="addend0", align_bytes=64),
-            reuse.tile([P, PACK, HALF], F32, name="addend1", offset=XS_ALL, align_bytes=64),
+            reuse.tile([P, PACK, HALF], F32, name="addend%d" % h, offset=W_RAW + 11 * N + 8 * N * h, align_bytes=64)
+            for h in range(2)
         ]
 
         def make_addend(h):
             for t in range(PACK):
-                if h == 0 or t >= GPSIMD_ROWS:
-                    nc.scalar.activation(
-                        out=addends[h][:, t, :],
-                        in_=shift_ps[:, h * HALF : (h + 1) * HALF],
-                        func=ACT.Identity,
-                        scale=g_cols[:, t : t + 1],
-                        bias=b_cols[:, t : t + 1],
-                    )
-                else:
-                    nc.gpsimd.tensor_scalar(
-                        out=addends[1][:, t, :],
-                        in0=shift_rows[:],
-                        scalar1=g_cols[:, t : t + 1],
-                        scalar2=b_cols[:, t : t + 1],
-                        op0=ALU.mult,
-                        op1=ALU.add,
-                    )
+                nc.scalar.activation(
+                    out=addends[h][:, t, :],
+                    in_=shift_ps[:, h * HALF : (h + 1) * HALF],
+                    func=ACT.Identity,
+                    scale=g_cols[:, t : t + 1],
+                    bias=b_cols[:, t : t + 1],
+                )
 
         y_codes = sb.tile([P, S], U32, name="y_codes", align_bytes=64)
         y_scales = sb.tile([P, S], U8, name="y_scales", align_bytes=64)

@@ -147,11 +147,10 @@ def tile_picked_lnfold_none_po_kernel(
         cast_w(1, slice(0, 2), nc.vector.tensor_copy)
         quantize_w(0)
         quantize_w(1)
+        inv_rows = reuse.tile([P, HALF], F32, name="inv_rows", offset=W_RAW + 8 * N + HALF, align_bytes=64)
+        nc.vector.tensor_copy(out=inv_rows[:], in_=inv_ps[:])
         xs_b = reuse.tile([P, HALF], U8, name="xs_b", offset=W_RAW + 8 * N, align_bytes=64)
         nc.vector.tensor_copy(xs_b[:], xs_all[:].indirect(half_offsets[1]))
-
-        inv_rows = reuse.tile([P, HALF], F32, name="inv_rows", offset=W_RAW + 8 * N + HALF, align_bytes=64)
-        nc.scalar.copy(out=inv_rows[:], in_=inv_ps[:])
 
         addends = [
             reuse.tile([P, PACK, HALF], F32, name="addend%d" % h, offset=W_RAW + 11 * N + 8 * N * h, align_bytes=64)

@@ -152,20 +152,15 @@ def tile_picked_lnfold_none_po_kernel(
         xs_b = reuse.tile([P, HALF], U8, name="xs_b", offset=W_RAW + 8 * N, align_bytes=64)
         nc.vector.tensor_copy(xs_b[:], xs_all[:].indirect(half_offsets[1]))
 
-        addends = [
-            reuse.tile([P, PACK, HALF], F32, name="addend%d" % h, offset=W_RAW + 11 * N + 8 * N * h, align_bytes=64)
-            for h in range(2)
-        ]
-
-        def make_addend(h):
-            for t in range(PACK):
-                nc.scalar.activation(
-                    out=addends[h][:, t, :],
-                    in_=shift_ps[:, h * HALF : (h + 1) * HALF],
-                    func=ACT.Identity,
-                    scale=g_cols[:, t : t + 1],
-                    bias=b_cols[:, t : t + 1],
-                )
+        addend = reuse.tile([P, PACK, S], F32, name="addend", offset=W_RAW + 11 * N, align_bytes=64)
+        for t in range(PACK):
+            nc.scalar.activation(
+                out=addend[:, t, :],
+                in_=shift_ps[:],
+                func=ACT.Identity,
+                scale=g_cols[:, t : t + 1],
+                bias=b_cols[:, t : t + 1],
+            )
 
         y_codes = sb.tile([P, S], U32, name="y_codes", align_bytes=64)
         y_scales = sb.tile([P, S], U8, name="y_scales", align_bytes=64)
@@ -176,7 +171,7 @@ def tile_picked_lnfold_none_po_kernel(
         scaled_a = []
         backs = []
         results = [result_a[:, :, c * CHUNK : (c + 1) * CHUNK] for c in range(DIRECT)]
-        roundeds = []
+        roundeds = [sb.tile([P, CHUNK, PACK], BF16, name="rounded%d" % c, align_bytes=64) for c in range(CHUNKS)]
 
         def scale_direct(u):
             acc = ps.tile([P, 2, HALF], F32, name="acc%d" % u, tag="acc%d" % u)
@@ -203,7 +198,7 @@ def tile_picked_lnfold_none_po_kernel(
         def finish_direct(u):
             pair = slice(2 * u, 2 * u + 2)
             nc.vector.tensor_tensor(
-                out=result_a[:, pair, :], in0=scaled_a[u][:], in1=addends[0][:, pair, :], op=ALU.add
+                out=result_a[:, pair, :], in0=scaled_a[u][:], in1=addend[:, pair, 0:HALF], op=ALU.add
             )
             nc.sync.dma_start(out=out_rows[:, pair, 0:HALF], in_=result_a[:, pair, :])
 
@@ -238,26 +233,23 @@ def tile_picked_lnfold_none_po_kernel(
 
         def finish_turned(c):
             cols = slice(c * CHUNK, (c + 1) * CHUNK)
-            in_half = slice(c * CHUNK - HALF, (c + 1) * CHUNK - HALF)
             result = sb.tile([P, PACK, CHUNK], F32, name="result%d" % c, align_bytes=64)
             for u in range(2):
                 pair = slice(2 * u, 2 * u + 2)
                 nc.vector.tensor_tensor(
                     out=result[:, pair, :],
                     in0=backs[2 * (c - DIRECT) + u][:],
-                    in1=addends[1][:, pair, in_half],
+                    in1=addend[:, pair, cols],
                     op=ALU.add,
                 )
             nc.sync.dma_start(out=out_rows[:, :, cols], in_=result[:])
             results.append(result[:])
 
-        def round_result(c, engine_copy):
-            rounded = sb.tile([P, CHUNK, PACK], BF16, name="rounded%d" % c, align_bytes=64)
+        def round_result(c, lo, hi, engine_copy):
             engine_copy(
-                out=rounded[:].rearrange("p (c i) t -> p c t i", i=4),
-                in_=results[c].rearrange("p t (c i) -> p c t i", i=4),
+                out=roundeds[c][:, lo:hi, :].rearrange("p (c i) t -> p c t i", i=4),
+                in_=results[c][:, :, lo:hi].rearrange("p t (c i) -> p c t i", i=4),
             )
-            roundeds.append(rounded)
 
         def planes(c):
             cols = slice(c * CHUNK, (c + 1) * CHUNK)
@@ -270,8 +262,6 @@ def tile_picked_lnfold_none_po_kernel(
         def store_words(queue, lo, hi):
             queue.dma_start(out=out_words[:, lo:hi], in_=y_codes[:, lo:hi].bitcast(I32))
 
-        make_addend(0)
-        make_addend(1)
         for u in range(2):
             scale_direct(u)
         for c in range(DIRECT, CHUNKS):
@@ -282,15 +272,17 @@ def tile_picked_lnfold_none_po_kernel(
             finish_direct(u)
         for c in range(DIRECT, CHUNKS):
             finish_turned(c)
-        for c in range(CHUNKS - 1):
-            round_result(c, nc.scalar.copy)
+        round_result(0, 0, CHUNK, nc.scalar.copy)
+        round_result(1, 0, CHUNK, nc.scalar.copy)
+        round_result(2, 0, CHUNK // 2, nc.scalar.copy)
         planes(0)
+        round_result(3, 0, CHUNK, nc.vector.tensor_copy)
+        round_result(2, CHUNK // 2, CHUNK, nc.vector.tensor_copy)
         planes(1)
-        round_result(CHUNKS - 1, nc.vector.tensor_copy)
-        planes(2)
+        store_words(nc.sync, 0, HALF)
         planes(3)
-        store_words(nc.sync, 0, S - CHUNK)
-        store_words(nc.scalar, S - CHUNK, S)
+        planes(2)
+        store_words(nc.scalar, HALF, S)
         for q in range(4):
             queue = nc.sync if q % 2 == 0 else nc.scalar
             queue.dma_start(

@@ -120,37 +120,42 @@ def tile_picked_lnfold_none_po_kernel(
                 shift_ps[:, c * CHUNK : (c + 1) * CHUNK], shift_col[:, c : c + 1].to_broadcast([P, P]), ident[:]
             )
 
-        w_bf = [
-            sb.tile([P, PACK, P // 2, PACK], BF16, name="w_bf0", align_bytes=64),
-            reuse.tile([P, PACK, P // 2, PACK], BF16, name="w_bf1", offset=W_BF1, align_bytes=64),
+        w_bf0 = sb.tile([P, PACK, P // 2, PACK], BF16, name="w_bf0", align_bytes=64)
+        w_bf1 = [
+            reuse.tile([P, 2, P // 2, PACK], BF16, name="w_bf1%d" % u, offset=W_BF1 + 2 * N * u, align_bytes=64)
+            for u in range(2)
         ]
         w_codes = sb.tile([P, N], U32, name="w_codes", align_bytes=64)
         w_scales = reuse.tile([P, N], U8, name="w_scales", offset=HALF, align_bytes=64)
+        w_dealt = [raw[:].rearrange("p j (m t) -> p m j t", t=PACK) for raw in w_raw]
+        nc.scalar.copy(out=w_bf0[:].rearrange("p t m j -> p m j t"), in_=w_dealt[0])
+        nc.scalar.copy(out=w_bf1[1][:].rearrange("p t m j -> p m j t"), in_=w_dealt[1][:, :, :, 2:4])
+        nc.vector.tensor_copy(out=w_bf1[0][:].rearrange("p t m j -> p m j t"), in_=w_dealt[1][:, :, :, 0:2])
+        for u in range(2):
+            for h in range(2):
+                for i in range(2):
+                    t = 2 * u + i
+                    cols = slice(t * P + h * P // 2, t * P + (h + 1) * P // 2)
+                    nc.vector.quantize_mx(
+                        out=w_codes[:, cols].bitcast(FP8X4),
+                        scales=w_scales[:, cols],
+                        in_=(w_bf0[:, t, :, :], w_bf1[u][:, i, :, :])[h].rearrange("p m j -> p (m j)"),
+                    )
 
-        def cast_w(h, tiles, engine_copy):
-            engine_copy(
-                out=w_bf[h][:, tiles, :, :].rearrange("p t m j -> p m j t"),
-                in_=w_raw[h][:].rearrange("p j (m t) -> p m j t", t=PACK)[:, :, :, tiles],
+        xs_turned = {}
+
+        def gather_scales(c):
+            xs_turned[c] = reuse.tile(
+                [P, CHUNK], U8, name="xs%d" % c, offset=W_RAW + 8 * N + CHUNK * (c - DIRECT), align_bytes=64
+            )
+            nc.vector.tensor_copy(
+                xs_turned[c][:], xs_all[:].indirect(offsets[:, c * CHUNK // 16 : (c + 1) * CHUNK // 16])
             )
 
-        def quantize_w(h):
-            for t in range(PACK):
-                cols = slice(t * P + h * P // 2, t * P + (h + 1) * P // 2)
-                nc.vector.quantize_mx(
-                    out=w_codes[:, cols].bitcast(FP8X4),
-                    scales=w_scales[:, cols],
-                    in_=w_bf[h][:, t, :, :].rearrange("p m j -> p (m j)"),
-                )
-
-        cast_w(0, slice(0, PACK), nc.scalar.copy)
-        cast_w(1, slice(2, PACK), nc.scalar.copy)
-        cast_w(1, slice(0, 2), nc.vector.tensor_copy)
-        quantize_w(0)
-        quantize_w(1)
+        gather_scales(2)
         inv_rows = reuse.tile([P, HALF], F32, name="inv_rows", offset=W_RAW + 8 * N + HALF, align_bytes=64)
         nc.vector.tensor_copy(out=inv_rows[:], in_=inv_ps[:])
-        xs_b = reuse.tile([P, HALF], U8, name="xs_b", offset=W_RAW + 8 * N, align_bytes=64)
-        nc.vector.tensor_copy(xs_b[:], xs_all[:].indirect(half_offsets[1]))
+        gather_scales(3)
 
         addend = reuse.tile([P, PACK, S], F32, name="addend", offset=W_RAW + 11 * N, align_bytes=64)
         for t in range(PACK):
@@ -210,7 +215,7 @@ def tile_picked_lnfold_none_po_kernel(
             nc.tensor.matmul_mx(
                 out=acc[:],
                 lhsT=xw_b[:, cols].bitcast(FP8X4),
-                lhsT_scale=xs_b[:, cols],
+                lhsT_scale=xs_turned[c][:],
                 rhs=w_codes[:].bitcast(FP8X4),
                 rhs_scale=w_scales[:],
                 start=True,

@@ -41,11 +41,13 @@ def tile_picked_lnfold_none_po_kernel(
         half_offsets = [offsets[:, h * HALF // 16 : (h + 1) * HALF // 16] for h in range(2)]
 
         stats = sb.tile([P, T], F32, name="stats", align_bytes=64)
-        nc.sync.dma_start(out=stats[MEAN_ROW:INV_ROW, :], in_=mean[0:1, :])
+        nc.scalar.dma_start(out=stats[MEAN_ROW:INV_ROW, :], in_=mean[0:1, :])
         nc.scalar.dma_start(out=stats[INV_ROW:P, :], in_=inv[0:1, :])
 
         xs_all = sb.tile([P, T], U8, name="xs_all", align_bytes=64)
         nc.gpsimd.memset(xs_all[:].bitcast(I32), 0)
+        warm = sb.tile([P, 16], F32, name="warm")
+        nc.vector.memset(warm[:, 0:1], 0.0)
         nc.vector.memset(stats[0:MEAN_ROW, :], 0.0)
 
         xw_all = sb.tile([P, T], U32, name="xw_all", align_bytes=64)
@@ -63,6 +65,8 @@ def tile_picked_lnfold_none_po_kernel(
 
         load_scales(nc.scalar, 0)
         load_scales(nc.scalar, 1)
+
+        nc.scalar.copy(out=warm[:, 8:9], in_=warm[:, 0:1])
 
         w_rows = w1.rearrange("(p j) c -> p j c", j=PACK)
         w_raw = []
@@ -86,8 +90,8 @@ def tile_picked_lnfold_none_po_kernel(
         nc.sync.dma_start(out=b_cols[:], in_=b.rearrange("(p t) o -> p (t o)", t=PACK))
 
         stats_g = reuse.tile([P, S], F32, name="stats_g", offset=0, align_bytes=64)
-        for h in range(2):
-            nc.vector.tensor_copy(stats_g[:, h * HALF : (h + 1) * HALF], stats[:].indirect(half_offsets[h]))
+        nc.vector.tensor_copy(stats_g[:, 0:HALF], stats[:].indirect(half_offsets[0]))
+        nc.scalar.activation(out=stats_g[:, HALF:S], in_=stats[:].indirect(half_offsets[1]), func=ACT.Copy)
         xw_g = sb.tile([P, S], U32, name="xw_g", align_bytes=64)
         nc.vector.tensor_copy(xw_g[:], xw_all[:].indirect(offsets[:]))
         xw_a, xw_b = xw_g[:, 0:HALF], xw_g[:, HALF:S]

@@ -20,7 +20,7 @@ CHUNK = 128
 CHUNKS = S // CHUNK
 HALF = S // 2
 DIRECT = CHUNKS // 2
-W_BF1 = 3 * HALF
+W_BF1 = 7 * CHUNK
 W_RAW = 8 * N
 MEAN_ROW, INV_ROW = 126, 127
 FLOPS = 2 * K * S * N
@@ -41,13 +41,13 @@ def tile_picked_lnfold_none_po_kernel(
         half_offsets = [offsets[:, h * HALF // 16 : (h + 1) * HALF // 16] for h in range(2)]
 
         stats = sb.tile([P, T], F32, name="stats", align_bytes=64)
-        nc.scalar.dma_start(out=stats[MEAN_ROW:INV_ROW, :], in_=mean[0:1, :])
+        nc.sync.dma_start(out=stats[MEAN_ROW:INV_ROW, :], in_=mean[0:1, :])
         nc.scalar.dma_start(out=stats[INV_ROW:P, :], in_=inv[0:1, :])
 
         xs_all = sb.tile([P, T], U8, name="xs_all", align_bytes=64)
         nc.gpsimd.memset(xs_all[:].bitcast(I32), 0)
-        warm = sb.tile([P, 16], F32, name="warm")
-        nc.vector.memset(warm[:, 0:1], 0.0)
+        signs = sb.tile([P, 2, CHUNKS], F32, name="signs")
+        nc.vector.memset(signs[:, 0, :], -1.0)
         nc.vector.memset(stats[0:MEAN_ROW, :], 0.0)
 
         xw_all = sb.tile([P, T], U32, name="xw_all", align_bytes=64)
@@ -66,7 +66,7 @@ def tile_picked_lnfold_none_po_kernel(
         load_scales(nc.scalar, 0)
         load_scales(nc.scalar, 1)
 
-        nc.scalar.copy(out=warm[:, 8:9], in_=warm[:, 0:1])
+        nc.scalar.activation(out=signs[:, 1, :], in_=signs[:, 0, :], func=ACT.Copy, scale=-1.0)
 
         w_rows = w1.rearrange("(p j) c -> p j c", j=PACK)
         w_raw = []
@@ -80,9 +80,6 @@ def tile_picked_lnfold_none_po_kernel(
 
         ident = sb.tile([P, P], F32, name="ident", align_bytes=64)
         make_identity(nc, ident[:])
-        signs = sb.tile([P, 2, CHUNKS], F32, name="signs")
-        nc.vector.memset(signs[:, 0, :], -1.0)
-        nc.vector.memset(signs[:, 1, :], 1.0)
 
         g_cols = sb.tile([P, PACK], F32, name="g_cols")
         b_cols = sb.tile([P, PACK], F32, name="b_cols")
@@ -110,8 +107,8 @@ def tile_picked_lnfold_none_po_kernel(
         shift_col = sb.tile([P, CHUNKS], F32, name="shift_col")
         nc.gpsimd.tensor_tensor(out=shift_col[:], in0=stat_cols[:, 0, :], in1=inv_col, op=ALU.mult)
 
-        xs_a = reuse.tile([P, HALF], U8, name="xs_a", offset=0, align_bytes=64)
-        nc.vector.tensor_copy(xs_a[:], xs_all[:].indirect(half_offsets[0]))
+        xs_a = reuse.tile([P, 3 * CHUNK], U8, name="xs_a", offset=0, align_bytes=64)
+        nc.vector.tensor_copy(xs_a[:], xs_all[:].indirect(offsets[:, 0 : 3 * CHUNK // 16]))
 
         inv_ps = ps.tile([P, HALF], F32, name="inv_ps", tag="inv")
         shift_ps = ps.tile([P, S], F32, name="shift_ps")
@@ -130,12 +127,14 @@ def tile_picked_lnfold_none_po_kernel(
             for u in range(2)
         ]
         w_codes = sb.tile([P, N], U32, name="w_codes", align_bytes=64)
-        w_scales = reuse.tile([P, N], U8, name="w_scales", offset=HALF, align_bytes=64)
+        w_scales = reuse.tile([P, N], U8, name="w_scales", offset=3 * CHUNK, align_bytes=64)
         w_dealt = [raw[:].rearrange("p j (m t) -> p m j t", t=PACK) for raw in w_raw]
         nc.scalar.copy(out=w_bf0[:].rearrange("p t m j -> p m j t"), in_=w_dealt[0])
-        nc.scalar.copy(out=w_bf1[1][:].rearrange("p t m j -> p m j t"), in_=w_dealt[1][:, :, :, 2:4])
-        nc.vector.tensor_copy(out=w_bf1[0][:].rearrange("p t m j -> p m j t"), in_=w_dealt[1][:, :, :, 0:2])
+        bf_dealt = [w[:].rearrange("p t m j -> p m j t") for w in w_bf1]
+        nc.scalar.copy(out=bf_dealt[1][:, 0 : P // 4], in_=w_dealt[1][:, 0 : P // 4, :, 2:4])
         for u in range(2):
+            lo = u * P // 4
+            nc.vector.tensor_copy(out=bf_dealt[u][:, lo : P // 2], in_=w_dealt[1][:, lo : P // 2, :, 2 * u : 2 * u + 2])
             for h in range(2):
                 for i in range(2):
                     t = 2 * u + i
@@ -146,7 +145,7 @@ def tile_picked_lnfold_none_po_kernel(
                         in_=(w_bf0[:, t, :, :], w_bf1[u][:, i, :, :])[h].rearrange("p m j -> p (m j)"),
                     )
 
-        xs_turned = {}
+        xs_turned = {2: xs_a[:, HALF : 3 * CHUNK]}
 
         def gather_scales(c):
             xs_turned[c] = reuse.tile(
@@ -156,12 +155,11 @@ def tile_picked_lnfold_none_po_kernel(
                 xs_turned[c][:], xs_all[:].indirect(offsets[:, c * CHUNK // 16 : (c + 1) * CHUNK // 16])
             )
 
-        gather_scales(2)
         inv_rows = reuse.tile([P, HALF], F32, name="inv_rows", offset=W_RAW + 8 * N + HALF, align_bytes=64)
         nc.vector.tensor_copy(out=inv_rows[:], in_=inv_ps[:])
         gather_scales(3)
 
-        addend = reuse.tile([P, PACK, S], F32, name="addend", offset=W_RAW + 11 * N, align_bytes=64)
+        addend = sb.tile([P, PACK, S], F32, name="addend", align_bytes=64)
         for t in range(PACK):
             nc.scalar.activation(
                 out=addend[:, t, :],
@@ -191,7 +189,7 @@ def tile_picked_lnfold_none_po_kernel(
                     lhsT=w_codes[:, t * P : (t + 1) * P].bitcast(FP8X4),
                     lhsT_scale=w_scales[:, t * P : (t + 1) * P],
                     rhs=xw_a.bitcast(FP8X4),
-                    rhs_scale=xs_a[:],
+                    rhs_scale=xs_a[:, 0:HALF],
                     start=True,
                     stop=True,
                 )

@@ -286,10 +286,9 @@ def tile_picked_lnfold_none_po_kernel(
         round_result(3, 0, CHUNK, nc.vector.tensor_copy)
         round_result(2, CHUNK // 2, CHUNK, nc.vector.tensor_copy)
         planes(1)
-        store_words(nc.sync, 0, HALF)
         planes(3)
         planes(2)
-        store_words(nc.scalar, HALF, S)
+        store_words(nc.scalar, 0, S)
         for q in range(4):
             queue = nc.sync if q % 2 == 0 else nc.scalar
             queue.dma_start(

from contextlib import ExitStack

import concourse.mybir as mybir
from concourse.masks import make_identity

F32 = mybir.dt.float32
BF16 = mybir.dt.bfloat16
I32 = mybir.dt.int32
U32 = mybir.dt.uint32
U16 = mybir.dt.uint16
U8 = mybir.dt.uint8
FP8X4 = mybir.dt.float8_e4m3fn_x4
ALU = mybir.AluOpType
ACT = mybir.ActivationFunctionType

K, T, S, N = 512, 1024, 512, 512
P = 128
PACK = 4
CHUNK = 128
CHUNKS = S // CHUNK
HALF = S // 2
DIRECT = CHUNKS // 2
W_BF1 = 7 * CHUNK
W_RAW = 8 * N
MEAN_ROW, INV_ROW = 126, 127
FLOPS = 2 * K * S * N
BYTES = 4 * P * T + 16 * T + 2 * 4 * T + 2 * 4 * N + 4 * K * N + 2 * S * 8 + 4 * N * S + N * S + 16 * S


def tile_picked_lnfold_none_po_kernel(
    tc, x_words, x_scales, mean, inv, gsum, b, w1, offs, out_0, out_1, out_2
):
    nc = tc.nc
    with ExitStack() as ctx:
        sb = ctx.enter_context(tc.tile_pool(name="sb", bufs=1))
        reuse = ctx.enter_context(tc.tile_pool(name="reuse", bufs=1))
        ps = ctx.enter_context(tc.psum_pool(name="ps", bufs=1))

        offsets = sb.tile([P, S // 16], U16, name="offsets")
        nc.sync.dma_start(offsets[:], offs)
        half_offsets = [offsets[:, h * HALF // 16 : (h + 1) * HALF // 16] for h in range(2)]

        stats = sb.tile([P, T], F32, name="stats", align_bytes=64)
        nc.sync.dma_start(out=stats[MEAN_ROW:INV_ROW, :], in_=mean[0:1, :])
        nc.scalar.dma_start(out=stats[INV_ROW:P, :], in_=inv[0:1, :])

        xs_all = sb.tile([P, T], U8, name="xs_all", align_bytes=64)
        nc.gpsimd.memset(xs_all[:].bitcast(I32), 0)
        signs = sb.tile([P, 2, CHUNKS], F32, name="signs")
        nc.vector.memset(signs[:, 0, :], -1.0)
        nc.vector.memset(stats[0:MEAN_ROW, :], 0.0)

        xw_all = sb.tile([P, T], U32, name="xw_all", align_bytes=64)
        nc.sync.dma_start(
            out=xw_all[:].bitcast(I32),
            in_=x_words[0].rearrange("p c r -> p (c r)").bitcast(I32),
        )


        def load_scales(queue, q):
            queue.dma_start(
                out=xs_all[32 * q : 32 * q + 4, :].bitcast(I32),
                in_=x_scales[0][4 * q : 4 * q + 4, :].bitcast(I32),
            )

        load_scales(nc.scalar, 0)
        load_scales(nc.scalar, 1)

        nc.scalar.activation(out=signs[:, 1, :], in_=signs[:, 0, :], func=ACT.Copy, scale=-1.0)

        w_rows = w1.rearrange("(p j) c -> p j c", j=PACK)
        w_raw = []
        for h in range(2):
            raw = reuse.tile([P, PACK, N // 2], F32, name="w_raw%d" % h, offset=W_RAW + 8 * N * h, align_bytes=64)
            nc.sync.dma_start(out=raw[:], in_=w_rows[:, :, h * N // 2 : (h + 1) * N // 2])
            w_raw.append(raw)
            if h == 0:
                load_scales(nc.sync, 2)
                load_scales(nc.sync, 3)

        ident = sb.tile([P, P], F32, name="ident", align_bytes=64)
        make_identity(nc, ident[:])

        g_cols = sb.tile([P, PACK], F32, name="g_cols")
        b_cols = sb.tile([P, PACK], F32, name="b_cols")
        nc.sync.dma_start(out=g_cols[:], in_=gsum.rearrange("(p t) o -> p (t o)", t=PACK))
        nc.sync.dma_start(out=b_cols[:], in_=b.rearrange("(p t) o -> p (t o)", t=PACK))

        stats_g = reuse.tile([P, S], F32, name="stats_g", offset=0, align_bytes=64)
        nc.vector.tensor_copy(stats_g[:, 0:HALF], stats[:].indirect(half_offsets[0]))
        nc.scalar.activation(out=stats_g[:, HALF:S], in_=stats[:].indirect(half_offsets[1]), func=ACT.Copy)
        xw_g = sb.tile([P, S], U32, name="xw_g", align_bytes=64)
        nc.vector.tensor_copy(xw_g[:], xw_all[:].indirect(offsets[:]))
        xw_a, xw_b = xw_g[:, 0:HALF], xw_g[:, HALF:S]

        turned = ps.tile([P, CHUNKS, P], F32, name="turned", tag="turn")
        for c in range(CHUNKS):
            nc.tensor.transpose(turned[:, c, :], stats_g[:, c * CHUNK : (c + 1) * CHUNK], ident[:])
        stat_cols = sb.tile([P, 2, CHUNKS], F32, name="stat_cols")
        nc.vector.tensor_tensor(
            out=stat_cols[:],
            in0=turned[:, :, MEAN_ROW:P].rearrange("p c s -> p s c"),
            in1=signs[:],
            op=ALU.mult,
        )
        inv_col = stat_cols[:, 1, :]
        shift_col = sb.tile([P, CHUNKS], F32, name="shift_col")
        nc.gpsimd.tensor_tensor(out=shift_col[:], in0=stat_cols[:, 0, :], in1=inv_col, op=ALU.mult)

        xs_a = reuse.tile([P, 3 * CHUNK], U8, name="xs_a", offset=0, align_bytes=64)
        nc.vector.tensor_copy(xs_a[:], xs_all[:].indirect(offsets[:, 0 : 3 * CHUNK // 16]))

        inv_ps = ps.tile([P, HALF], F32, name="inv_ps", tag="inv")
        shift_ps = ps.tile([P, S], F32, name="shift_ps")
        for c in range(DIRECT):
            nc.tensor.transpose(
                inv_ps[:, c * CHUNK : (c + 1) * CHUNK], inv_col[:, c : c + 1].to_broadcast([P, P]), ident[:]
            )
        for c in range(CHUNKS):
            nc.tensor.transpose(
                shift_ps[:, c * CHUNK : (c + 1) * CHUNK], shift_col[:, c : c + 1].to_broadcast([P, P]), ident[:]
            )

        w_bf0 = sb.tile([P, PACK, P // 2, PACK], BF16, name="w_bf0", align_bytes=64)
        w_bf1 = [
            reuse.tile([P, 2, P // 2, PACK], BF16, name="w_bf1%d" % u, offset=W_BF1 + 2 * N * u, align_bytes=64)
            for u in range(2)
        ]
        w_codes = sb.tile([P, N], U32, name="w_codes", align_bytes=64)
        w_scales = reuse.tile([P, N], U8, name="w_scales", offset=3 * CHUNK, align_bytes=64)
        w_dealt = [raw[:].rearrange("p j (m t) -> p m j t", t=PACK) for raw in w_raw]
        nc.scalar.copy(out=w_bf0[:].rearrange("p t m j -> p m j t"), in_=w_dealt[0])
        bf_dealt = [w[:].rearrange("p t m j -> p m j t") for w in w_bf1]
        nc.scalar.copy(out=bf_dealt[1][:, 0 : P // 4], in_=w_dealt[1][:, 0 : P // 4, :, 2:4])
        for u in range(2):
            lo = u * P // 4
            nc.vector.tensor_copy(out=bf_dealt[u][:, lo : P // 2], in_=w_dealt[1][:, lo : P // 2, :, 2 * u : 2 * u + 2])
            for h in range(2):
                for i in range(2):
                    t = 2 * u + i
                    cols = slice(t * P + h * P // 2, t * P + (h + 1) * P // 2)
                    nc.vector.quantize_mx(
                        out=w_codes[:, cols].bitcast(FP8X4),
                        scales=w_scales[:, cols],
                        in_=(w_bf0[:, t, :, :], w_bf1[u][:, i, :, :])[h].rearrange("p m j -> p (m j)"),
                    )

        xs_turned = {2: xs_a[:, HALF : 3 * CHUNK]}

        def gather_scales(c):
            xs_turned[c] = reuse.tile(
                [P, CHUNK], U8, name="xs%d" % c, offset=W_RAW + 8 * N + CHUNK * (c - DIRECT), align_bytes=64
            )
            nc.vector.tensor_copy(
                xs_turned[c][:], xs_all[:].indirect(offsets[:, c * CHUNK // 16 : (c + 1) * CHUNK // 16])
            )

        inv_rows = reuse.tile([P, HALF], F32, name="inv_rows", offset=W_RAW + 8 * N + HALF, align_bytes=64)
        nc.vector.tensor_copy(out=inv_rows[:], in_=inv_ps[:])
        gather_scales(3)

        addend = sb.tile([P, PACK, S], F32, name="addend", align_bytes=64)
        for t in range(PACK):
            nc.scalar.activation(
                out=addend[:, t, :],
                in_=shift_ps[:],
                func=ACT.Identity,
                scale=g_cols[:, t : t + 1],
                bias=b_cols[:, t : t + 1],
            )

        y_codes = sb.tile([P, S], U32, name="y_codes", align_bytes=64)
        y_scales = sb.tile([P, S], U8, name="y_scales", align_bytes=64)
        out_rows = out_0.rearrange("(p t) j -> p t j", t=PACK)
        out_words = out_1[0].rearrange("p c r -> p (c r)").bitcast(I32)

        result_a = sb.tile([P, PACK, HALF], F32, name="result_a", align_bytes=64)
        scaled_a = []
        backs = []
        results = [result_a[:, :, c * CHUNK : (c + 1) * CHUNK] for c in range(DIRECT)]
        roundeds = [sb.tile([P, CHUNK, PACK], BF16, name="rounded%d" % c, align_bytes=64) for c in range(CHUNKS)]

        def scale_direct(u):
            acc = ps.tile([P, 2, HALF], F32, name="acc%d" % u, tag="acc%d" % u)
            for i in range(2):
                t = 2 * u + i
                nc.tensor.matmul_mx(
                    out=acc[:, i, :],
                    lhsT=w_codes[:, t * P : (t + 1) * P].bitcast(FP8X4),
                    lhsT_scale=w_scales[:, t * P : (t + 1) * P],
                    rhs=xw_a.bitcast(FP8X4),
                    rhs_scale=xs_a[:, 0:HALF],
                    start=True,
                    stop=True,
                )
            z = sb.tile([P, 2, HALF], F32, name="scaled%d" % u, align_bytes=64)
            nc.vector.tensor_tensor(
                out=z[:],
                in0=acc[:],
                in1=inv_rows[:].unsqueeze(1).to_broadcast([P, 2, HALF]),
                op=ALU.mult,
            )
            scaled_a.append(z)

        def finish_direct(u):
            pair = slice(2 * u, 2 * u + 2)
            nc.vector.tensor_tensor(
                out=result_a[:, pair, :], in0=scaled_a[u][:], in1=addend[:, pair, 0:HALF], op=ALU.add
            )
            nc.sync.dma_start(out=out_rows[:, pair, 0:HALF], in_=result_a[:, pair, :])

        by_token = []

        def scale_turned(c):
            cols = slice(c * CHUNK - HALF, (c + 1) * CHUNK - HALF)
            acc = ps.tile([P, N], F32, name="acc%d" % c)
            nc.tensor.matmul_mx(
                out=acc[:],
                lhsT=xw_b[:, cols].bitcast(FP8X4),
                lhsT_scale=xs_turned[c][:],
                rhs=w_codes[:].bitcast(FP8X4),
                rhs_scale=w_scales[:],
                start=True,
                stop=True,
            )
            z = sb.tile([P, N], F32, name="by_token%d" % c, align_bytes=64)
            for u in range(2):
                pair = slice(u * N // 2, (u + 1) * N // 2)
                nc.scalar.activation(out=z[:, pair], in_=acc[:, pair], func=ACT.Copy, scale=inv_col[:, c : c + 1])
            by_token.append(z)

        def turn_back(c):
            for u in range(2):
                tag = ("turn", "inv", "back", "acc0")[2 * (c - DIRECT) + u]
                back = ps.tile([P, 2, CHUNK], F32, name="back%d%d" % (c, u), tag=tag)
                for i in range(2):
                    t = 2 * u + i
                    nc.tensor.transpose(back[:, i, :], by_token[c - DIRECT][:, t * P : (t + 1) * P], ident[:])
                backs.append(back)

        def finish_turned(c):
            cols = slice(c * CHUNK, (c + 1) * CHUNK)
            result = sb.tile([P, PACK, CHUNK], F32, name="result%d" % c, align_bytes=64)
            for u in range(2):
                pair = slice(2 * u, 2 * u + 2)
                nc.vector.tensor_tensor(
                    out=result[:, pair, :],
                    in0=backs[2 * (c - DIRECT) + u][:],
                    in1=addend[:, pair, cols],
                    op=ALU.add,
                )
            nc.sync.dma_start(out=out_rows[:, :, cols], in_=result[:])
            results.append(result[:])

        def round_result(c, lo, hi, engine_copy):
            engine_copy(
                out=roundeds[c][:, lo:hi, :].rearrange("p (c i) t -> p c t i", i=4),
                in_=results[c][:, :, lo:hi].rearrange("p t (c i) -> p c t i", i=4),
            )

        def planes(c):
            cols = slice(c * CHUNK, (c + 1) * CHUNK)
            nc.vector.quantize_mx(
                out=y_codes[:, cols].bitcast(FP8X4),
                scales=y_scales[:, cols],
                in_=roundeds[c][:].rearrange("p c t -> p (c t)"),
            )

        def store_words(queue, lo, hi):
            queue.dma_start(out=out_words[:, lo:hi], in_=y_codes[:, lo:hi].bitcast(I32))

        for u in range(2):
            scale_direct(u)
        for c in range(DIRECT, CHUNKS):
            scale_turned(c)
        for c in range(DIRECT, CHUNKS):
            turn_back(c)
        for u in range(2):
            finish_direct(u)
        for c in range(DIRECT, CHUNKS):
            finish_turned(c)
        round_result(0, 0, CHUNK, nc.scalar.copy)
        round_result(1, 0, CHUNK, nc.scalar.copy)
        round_result(2, 0, CHUNK // 2, nc.scalar.copy)
        planes(0)
        round_result(3, 0, CHUNK, nc.vector.tensor_copy)
        round_result(2, CHUNK // 2, CHUNK, nc.vector.tensor_copy)
        planes(1)
        planes(3)
        planes(2)
        store_words(nc.scalar, 0, S)
        for q in range(4):
            queue = nc.sync if q % 2 == 0 else nc.scalar
            queue.dma_start(
                out=out_2[0][4 * q : 4 * q + 4, :].bitcast(I32),
                in_=y_scales[32 * q : 32 * q + 4, :].bitcast(I32),
            )
